import numpy as np
import ml_dtypes


def mxq(x, axis, fmt="e4m3"):
    dtype, down = {"e4m3": (ml_dtypes.float8_e4m3fn, 7), "e5m2": (ml_dtypes.float8_e5m2, 14)}[fmt]
    v = np.moveaxis(np.asarray(x, np.float32).astype(ml_dtypes.bfloat16).astype(np.float64), axis, -1)
    blocks = v.reshape(v.shape[:-1] + (-1, 32))
    amax = np.abs(blocks).max(-1, keepdims=True)
    byte = np.maximum(np.where(amax > 0, np.frexp(amax)[1] - 1 + 127, 0) - down, 1)
    scale = np.exp2(byte - 127.0)
    codes = (blocks / scale).astype(np.float32).astype(dtype).astype(np.float64)
    return np.moveaxis((codes * scale).reshape(v.shape), -1, axis)


WIDE = False


def mx_kscale(k):
    if not WIDE:
        return np.ones(k)
    levels = np.array([10, -10, 5, -5, 0])
    if k % 512:
        return np.exp2(np.random.permutation(np.resize(levels, k // 32))).repeat(32)
    a = np.empty((k // 512, 16))
    for p in range(k // 512):
        a[p, :8] = np.random.permutation(np.resize(levels, 8))
        for g in range(8):
            far = levels[np.abs(levels - a[p, g]) >= 10]
            a[p, g + 8] = far[np.random.randint(len(far))]
    return np.exp2(a.ravel()).repeat(32)


def f64(x):
    return np.asarray(x).astype(np.float64)


def striped(idx):
    return np.tile(np.asarray(idx).reshape(-1, 16).T, (8, 1)).astype(np.uint16)


def unstriped(offs):
    return offs[:16].T.reshape(-1).astype(np.int64)


E2M1 = np.array([0.0, 0.5, 1.0, 1.5, 2.0, 3.0, 4.0, 6.0, -0.0, -0.5, -1.0, -1.5, -2.0, -3.0, -4.0, -6.0])


def pack_weight(w, fmt):
    k, n = w.shape
    w = f64(np.asarray(w, np.float32).astype(ml_dtypes.bfloat16)).reshape(k // 32, 32, n)
    amax = np.abs(w).max(1)
    if fmt == "e4m3":
        byte = np.frexp(amax)[1] - 1 + 127 - 7
    else:
        mant, ex = np.frexp(amax / 6.0)
        byte = np.where(mant > 0.5, ex, ex - 1) + 127
    byte = np.clip(np.where(amax > 0, byte, 1), 1, 254)
    scaled = (w * np.exp2(127.0 - byte)[:, None, :]).reshape(k, n).astype(np.float32)
    by_word = np.ascontiguousarray(scaled.reshape(k // 512, 128, 4, n).transpose(0, 1, 3, 2))
    if fmt == "e4m3":
        words = by_word.astype(ml_dtypes.float8_e4m3fn).view(np.uint8)
    else:
        c = by_word.astype(ml_dtypes.float4_e2m1fn).view(np.uint8) & 0xF
        words = (c[..., 0::2] | (c[..., 1::2] << 4)).reshape(k // 512, 128, 2 * n)
    return np.ascontiguousarray(words), np.ascontiguousarray(byte.astype(np.uint8).reshape(k // 512, 16, n))


def unpack_weight(words, scales, fmt):
    g, _, n = scales.shape
    words = np.ascontiguousarray(words).reshape(g, 128, n, -1)
    if fmt == "e4m3":
        vals = words.view(ml_dtypes.float8_e4m3fn).astype(np.float64)
    else:
        nib = np.empty((g, 128, n, 4), np.uint8)
        nib[..., 0::2] = words & 0xF
        nib[..., 1::2] = words >> 4
        vals = E2M1[nib]
    vals = vals * np.repeat(np.exp2(scales.astype(np.float64) - 127.0), 8, axis=1)[..., None]
    return vals.transpose(0, 1, 3, 2).reshape(g * 512, n)


def softplus(v):
    return np.log(1.0 + np.exp(v))


def sigmoid(v):
    return 1.0 / (1.0 + np.exp(-v))


def bf(x):
    return np.asarray(x, np.float32).astype(ml_dtypes.bfloat16)


def planes(Y):
    r, m = Y.shape
    b = f64(bf(Y)).reshape(r // 32, 32, m)
    amax = np.abs(b).max(1)
    byte = np.clip(np.where(amax > 0, np.frexp(amax)[1] - 1 + 127 - 7, 1), 1, 254)
    codes = (b * np.exp2(127.0 - byte)[:, None, :]).reshape(r, m).astype(np.float32).astype(ml_dtypes.float8_e4m3fn).view(np.uint8)
    words = codes.reshape(r // 512, 128, 4, m).transpose(0, 1, 3, 2)
    return np.ascontiguousarray(words), np.ascontiguousarray(byte.astype(np.uint8).reshape(r // 512, 16, m))


D, E, T, I, Q = 512, 512, 2048, 512, 256


def setup_inputs():
    n = np.random.standard_normal
    idx = np.random.permutation(T)[:I]
    fd = mx_kscale(D)
    fi = mx_kscale(I)
    ti = np.ones(T)
    ti[idx] = fi
    keysp = pack_weight(n((D, T)) / fd[:, None], "e2m1")
    return {
        "query": (n((D, Q)) * 1.0 / np.sqrt(D) * fd[:, None]).astype(np.float32),
        "dquery": (n((D, Q)) * 1.0 / np.sqrt(D) * fd[:, None]).astype(np.float32),
        "keys_words": keysp[0],
        "keys_scales": keysp[1],
        "th": (np.random.uniform(-0.5, 0.5, (Q, 1))).astype(np.float32),
        "reserve": (np.random.uniform(20.0, 100.0, (Q, 1))).astype(np.float32),
        "os": (np.random.uniform(4.0, 16.0, (1, I)) * fi).astype(np.float32),
        "vals": (n((E, T)) / ti).astype(np.float32),
        "offs": striped(idx),
    }


def reference(query, dquery, keys_words, keys_scales, th, reserve, os, vals, offs):
    idx = unstriped(offs)
    keysu = unpack_weight(keys_words, keys_scales, "e2m1")
    queryq = mxq(f64(query), 0, "e4m3")
    keysidxg = keysu[:, idx]
    a = queryq.T @ keysidxg
    dqueryq = mxq(f64(dquery), 0, "e4m3")
    ta = dqueryq.T @ keysidxg
    p = softplus(a - f64(th))
    tp = ta * sigmoid(a - f64(th))
    tw = (tp - np.sum(tp, axis=1, keepdims=True) * p / (np.sum(p, axis=1, keepdims=True) + f64(reserve))) / (np.sum(p, axis=1, keepdims=True) + f64(reserve))
    wo1 = tw * f64(os)
    wt1 = wo1.T
    vt1 = f64(vals)[:, idx].T
    vt1q = mxq(vt1, 0, "e4m3")
    wt1q = mxq(wt1, 0, "e4m3")
    o = vt1q.T @ wt1q
    words, scales = planes(o)
    return o, words, scales

@@ -1,0 +1,268 @@
+from contextlib import ExitStack
+
+import concourse.mybir as mybir
+
+D, E, T, I, Q = 512, 512, 2048, 512, 256
+FLOPS = 2 * (2 * D * Q * I + I * E * Q)
+
+F32 = mybir.dt.float32
+BF16 = mybir.dt.bfloat16
+I32 = mybir.dt.int32
+U32 = mybir.dt.uint32
+U16 = mybir.dt.uint16
+U8 = mybir.dt.uint8
+FP8X4 = mybir.dt.float8_e4m3fn_x4
+FP4X4 = mybir.dt.float4_e2m1fn_x4
+ALU = mybir.AluOpType
+ACT = mybir.ActivationFunctionType
+
+P = 128
+PACK = 4
+BLOCKS = Q // P
+QUADRANTS = 4
+FLOOR = -40.0
+POOL_BYTES = T * 4
+
+
+def tile_attend_ttsoftthreshold_pl_kernel(
+    tc, query, dquery, keys_words, keys_scales, th, reserve, slot_factor, vals, offs, out_0, out_1, out_2
+):
+    nc = tc.nc
+    with ExitStack() as ctx:
+        held = ctx.enter_context(tc.tile_pool(name="held", bufs=1))
+        reuse = ctx.enter_context(tc.tile_pool(name="reuse", bufs=1))
+        psum = ctx.enter_context(tc.psum_pool(name="psum", bufs=2))
+
+        def sbuf(name, shape, dtype):
+            return held.tile(shape, dtype, name=name, align_bytes=64)
+
+        def placed(region, at, name, shape, dtype):
+            return reuse.tile(shape, dtype, name=name, align_bytes=64, offset=region * POOL_BYTES + at)
+
+        def per_block(name, shape, dtype):
+            return [sbuf("%s%d" % (name, b), shape, dtype) for b in range(BLOCKS)]
+
+        def cols(b):
+            return slice(b * P, (b + 1) * P)
+
+        offsets = held.tile([P, I // 16], U16, name="offsets")
+        nc.sync.dma_start(offsets[:], offs)
+        key_word_pool = sbuf("key_word_pool", [P, T], U16)
+        nc.sync.dma_start(key_word_pool[:].bitcast(I32), keys_words[0].bitcast(I32))
+        key_scale_pool = sbuf("key_scale_pool", [P, T], U8)
+        nc.gpsimd.memset(key_scale_pool[:].bitcast(I32), 0)
+        for quad in range(QUADRANTS):
+            nc.sync.dma_start(
+                key_scale_pool[32 * quad : 32 * quad + 4, :].bitcast(I32),
+                keys_scales[0, 4 * quad : 4 * quad + 4, :].bitcast(I32),
+            )
+        zeros = placed(0, 0, "zeros", [P, 7 * T], F32)
+        nc.vector.memset(zeros[:, :P], 0.0)
+        identity = sbuf("identity", [P, P], F32)
+        nc.gpsimd.affine_select(
+            out=identity[:], in_=zeros[:, :P], compare_op=ALU.not_equal, fill=1.0, base=0,
+            pattern=[[-1, P]], channel_multiplier=1,
+        )
+        floor = placed(7, 0, "floor", [P, 1], F32)
+        nc.vector.memset(floor[:], FLOOR)
+        warm = sbuf("warm", [P, 1], F32)
+        nc.scalar.activation(warm[:], floor[:], ACT.Sigmoid)
+
+        query_raw = placed(5, 4096, "query_raw", [P, PACK, Q], F32)
+        nc.sync.dma_start(query_raw[:], query.rearrange("(p t) q -> p t q", t=PACK))
+        dquery_raw = placed(5, 0, "dquery_raw", [P, PACK, Q], F32)
+        nc.sync.dma_start(dquery_raw[:], dquery.rearrange("(p t) q -> p t q", t=PACK))
+        val_pool = [placed(j, 0, "val_pool%d" % j, [P, T], F32) for j in range(PACK)]
+        vals_dealt = vals.rearrange("(m j) t -> m j t", j=PACK)
+        th_cols = placed(6, 0, "th_cols", [P, BLOCKS], F32)
+        reserve_cols = placed(6, 64, "reserve_cols", [P, BLOCKS], F32)
+        factor_cols = placed(6, 128, "factor_cols", [P, PACK], F32)
+        with nc.allow_non_contiguous_dma(reason="one value a partition and row block"):
+            nc.sync.dma_start(th_cols[:], th.rearrange("(b p) o -> p (b o)", p=P))
+            nc.sync.dma_start(val_pool[0][:], vals_dealt[:, 0, :])
+            nc.sync.dma_start(reserve_cols[:], reserve.rearrange("(b p) o -> p (b o)", p=P))
+        nc.sync.dma_start(val_pool[1][:], vals_dealt[:, 1, :])
+        nc.sync.dma_start(factor_cols[:], slot_factor.rearrange("o (p t) -> p (o t)", t=PACK))
+        for j in range(2, PACK):
+            nc.sync.dma_start(val_pool[j][:], vals_dealt[:, j, :])
+
+        def round_and_interleave(name, raw):
+            grouped = sbuf(name, [P, raw.shape[2], PACK], BF16)
+            nc.scalar.copy(
+                grouped[:].rearrange("p (c i) t -> p c t i", i=4),
+                raw.rearrange("p t (c i) -> p c t i", i=4),
+            )
+            return grouped
+
+        def quantise(name, grouped, codes):
+            scales = sbuf(name + "_scales", [P, codes.shape[1]], U8)
+            nc.vector.quantize_mx(codes[:].bitcast(FP8X4), scales[:], grouped[:].rearrange("p c t -> p (c t)"))
+            return codes, scales
+
+        key_words = sbuf("key_words", [P, I], U16)
+        nc.vector.tensor_copy(key_words[:], key_word_pool[:].indirect(offsets[:]))
+        key_scales = sbuf("key_scales", [P, I], U8)
+        nc.vector.tensor_copy(key_scales[:], key_scale_pool[:].indirect(offsets[:]))
+        query_mx = [
+            quantise(
+                "query%d" % b,
+                round_and_interleave("query_grouped%d" % b, query_raw[:, :, cols(b)]),
+                sbuf("query_codes%d" % b, [P, P], U32),
+            )
+            for b in range(BLOCKS)
+        ]
+        dquery_grouped = round_and_interleave("dquery_grouped", dquery_raw[:])
+
+        def scores(codes, scales, tag):
+            bank = psum.tile([P, I], F32, name=tag, tag=tag)
+            nc.tensor.matmul_mx(
+                bank[:],
+                lhsT=codes.bitcast(FP8X4),
+                lhsT_scale=scales,
+                rhs=key_words[:].bitcast(FP4X4),
+                rhs_scale=key_scales[:],
+                start=True,
+                stop=True,
+            )
+            return bank[:].rearrange("q (s r) -> q r s", r=PACK)
+
+        x = per_block("x", [P, PACK, P], F32)
+        x_sum = per_block("x_sum", [P, 1], F32)
+        x_sum_reserve = per_block("x_sum_reserve", [P, 1], F32)
+        sig = [placed(5, 0, "sig0", [P, PACK, P], F32), placed(PACK, 2048, "sig1", [P, PACK, P], F32)]
+        log_sig = per_block("log_sig", [P, PACK, P], F32)
+        log_sig_sum = per_block("log_sig_sum", [P, 1], F32)
+        denom = [placed(7, 2048 + 1024 * b, "denom%d" % b, [P, 1], F32) for b in range(BLOCKS)]
+        neg_part = [placed(PACK, 4096 + 2048 * b, "neg_part%d" % b, [P, PACK, P], F32) for b in range(BLOCKS)]
+        tp = per_block("tp", [P, PACK, P], F32)
+        first_sum = per_block("first_sum", [P, 1], F32)
+        first = per_block("first", [P, PACK, P], F32)
+        second_scale = per_block("second_scale", [P, 1], F32)
+        second = per_block("second", [P, PACK, P], F32)
+
+        a = [scores(codes[:], scales[:], "score") for codes, scales in query_mx]
+        for b in range(BLOCKS):
+            nc.vector.scalar_tensor_tensor(
+                x[b][:], a[b], th_cols[:, b : b + 1], floor[:].unsqueeze(1).to_broadcast([P, PACK, P]),
+                ALU.subtract, ALU.max, accum_out=x_sum[b][:],
+            )
+            nc.scalar.activation(sig[b][:], x[b][:], ACT.Sigmoid)
+            nc.gpsimd.tensor_tensor(x_sum_reserve[b][:], x_sum[b][:], reserve_cols[:, b : b + 1], ALU.add)
+
+        dquery_codes, dquery_scales = quantise("dquery", dquery_grouped, placed(7, 1024, "dquery_codes", [P, Q], U32))
+        ta = [scores(dquery_codes[:, cols(b)], dquery_scales[:, cols(b)], "dscore") for b in range(BLOCKS)]
+
+        def gather_values(picked, j):
+            nc.vector.tensor_copy(picked[:], val_pool[j][:].indirect(offsets[:]))
+            words = picked[:].bitcast(F32)
+            turned = psum.tile([P, 2, P], F32, name="turned", tag="turned", bufs=4)
+            for u in range(2):
+                nc.tensor.transpose(turned[:, u, :], words[:, u::2], identity[:])
+            return turned
+
+        def group_values(grouped, turned):
+            nc.scalar.copy(grouped[:].bitcast(F32), turned[:].rearrange("p u m -> p m u"))
+
+        turned0 = gather_values(placed(7, 0, "picked0", [P, I], BF16), 0)
+        for b in range(BLOCKS):
+            nc.vector.tensor_tensor(tp[b][:], ta[b], sig[b][:], ALU.mult)
+        for b in range(BLOCKS):
+            nc.scalar.activation(log_sig[b][:], sig[b][:], ACT.Ln, accum_out=log_sig_sum[b][:])
+            nc.scalar.activation(
+                denom[b][:], log_sig_sum[b][:], ACT.Identity, bias=x_sum_reserve[b][:], scale=-1.0
+            )
+            nc.gpsimd.tensor_tensor(neg_part[b][:], log_sig[b][:], x[b][:], ALU.subtract)
+
+        val_grouped0 = placed(PACK, 2048, "val_grouped0", [P, P, PACK], BF16)
+        group_values(val_grouped0, turned0)
+        turned1 = gather_values(placed(7, 1024, "picked1", [P, I], BF16), 1)
+        inv_denom = [placed(1, 64 * b, "inv_denom%d" % b, [P, 1], F32) for b in range(BLOCKS)]
+        for b in range(BLOCKS):
+            nc.vector.reciprocal(inv_denom[b][:], denom[b][:])
+        val0_mx = quantise("val0", val_grouped0, placed(7, 2048, "val0_codes", [P, P], U32))
+        turned2 = gather_values(placed(7, 3072, "picked2", [P, I], BF16), 2)
+
+        weights_turned = []
+        for b in range(BLOCKS):
+            nc.scalar.activation(first[b][:], tp[b][:], ACT.Copy, scale=inv_denom[b][:], accum_out=first_sum[b][:])
+            nc.scalar.activation(second_scale[b][:], first_sum[b][:], ACT.Copy, scale=inv_denom[b][:])
+            nc.scalar.activation(second[b][:], neg_part[b][:], ACT.Copy, scale=second_scale[b][:])
+            bank = psum.tile([P, PACK, P], F32, name="score", tag="score")
+            terms = [(term, r) for term in (first[b], second[b]) for r in range(PACK)]
+            for n, (term, r) in enumerate(terms):
+                nc.tensor.matmul(
+                    bank[:, r, :], term[:, r, :], identity[:],
+                    start=(n == 0), stop=(n == len(terms) - 1), is_transpose=True,
+                )
+            weights_turned.append(bank)
+
+        def weigh(grouped, b):
+            nc.vector.tensor_tensor(
+                grouped[:],
+                weights_turned[b][:].rearrange("s r q -> s q r"),
+                factor_cols[:].unsqueeze(1).to_broadcast([P, P, PACK]),
+                ALU.mult,
+            )
+            return grouped
+
+        middle_grouped = placed(PACK, 4096 + 2048, "middle_grouped", [P, 2 * P, PACK], BF16)
+        group_values(middle_grouped[:, cols(0), :], turned1)
+        group_values(middle_grouped[:, cols(1), :], turned2)
+        weights_grouped0 = weigh(placed(7, 4096, "weights_grouped0", [P, P, PACK], BF16), 0)
+        weights_mx = [quantise("weights0", weights_grouped0, sbuf("weights0_codes", [P, P], U32))]
+        val_grouped3 = sbuf("val_grouped3", [P, P, PACK], BF16)
+        group_values(val_grouped3, gather_values(placed(7, 4096, "picked3", [P, I], BF16), 3))
+        weights_grouped1 = weigh(placed(3, 0, "weights_grouped1", [P, P, PACK], BF16), 1)
+        middle_codes, middle_scales = quantise("middle", middle_grouped, placed(3, 1024, "middle_codes", [P, 2 * P], U32))
+        weights_mx.append(quantise("weights1", weights_grouped1, sbuf("weights1_codes", [P, P], U32)))
+        val_mx = [val0_mx] + [(middle_codes[:, cols(j)], middle_scales[:, cols(j)]) for j in range(2)]
+
+        result = [psum.tile([P, PACK, P], F32, name="result", tag="dscore") for b in range(BLOCKS)]
+        staged = per_block("staged", [P, PACK, P], F32)
+        out_dealt = out_0.rearrange("(m j) q -> m j q", j=PACK)
+
+        def product(j, b):
+            nc.tensor.matmul_mx(
+                result[b][:, j, :],
+                lhsT=val_mx[j][0][:].bitcast(FP8X4),
+                lhsT_scale=val_mx[j][1][:],
+                rhs=weights_mx[b][0][:].bitcast(FP8X4),
+                rhs_scale=weights_mx[b][1][:],
+                start=True,
+                stop=True,
+            )
+
+        last = PACK - 1
+        for b in range(BLOCKS):
+            for j in range(last):
+                product(j, b)
+        nc.scalar.copy(staged[0][:, :last, :], result[0][:, :last, :])
+        val_mx.append(quantise("val3", val_grouped3, sbuf("val3_codes", [P, P], U32)))
+        product(last, 1)
+        product(last, 0)
+        nc.scalar.copy(staged[1][:], result[1][:])
+        nc.vector.tensor_copy(staged[0][:, last, :], result[0][:, last, :])
+        nc.sync.dma_start(out_dealt[:, :, cols(0)], staged[0][:])
+        nc.scalar.dma_start(out_dealt[:, :, cols(1)], staged[1][:])
+
+        out_codes = sbuf("out_codes", [P, Q], U32)
+        out_scales = sbuf("out_scales", [P, Q], U8)
+        out_grouped = per_block("out_grouped", [P, P, PACK], BF16)
+        for b in range(BLOCKS):
+            nc.vector.tensor_copy(
+                out_grouped[b][:].rearrange("m (c i) j -> m c j i", i=4),
+                staged[b][:].rearrange("m j (c i) -> m c j i", i=4),
+            )
+        for b in range(BLOCKS):
+            nc.vector.quantize_mx(
+                out_codes[:, cols(b)].bitcast(FP8X4),
+                out_scales[:, cols(b)],
+                out_grouped[b][:].rearrange("m q j -> m (q j)"),
+            )
+        nc.sync.dma_start(out_1[0].rearrange("p c t -> p (c t)").bitcast(I32), out_codes[:].bitcast(I32))
+        for quad in range(QUADRANTS):
+            queue = nc.sync if quad % 2 == 0 else nc.scalar
+            queue.dma_start(
+                out_2[0, 4 * quad : 4 * quad + 4, :].bitcast(I32),
+                out_scales[32 * quad : 32 * quad + 4, :].bitcast(I32),
+            )

@@ -74,17 +74,15 @@ def tile_attend_ttsoftthreshold_pl_kernel(
         nc.sync.dma_start(dquery_raw[:], dquery.rearrange("(p t) q -> p t q", t=PACK))
         val_pool = [placed(j, 0, "val_pool%d" % j, [P, T], F32) for j in range(PACK)]
         vals_dealt = vals.rearrange("(m j) t -> m j t", j=PACK)
-        th_cols = placed(6, 0, "th_cols", [P, BLOCKS], F32)
-        reserve_cols = placed(6, 64, "reserve_cols", [P, BLOCKS], F32)
-        factor_cols = placed(6, 128, "factor_cols", [P, PACK], F32)
-        with nc.allow_non_contiguous_dma(reason="one value a partition and row block"):
-            nc.sync.dma_start(th_cols[:], th.rearrange("(b p) o -> p (b o)", p=P))
-            nc.sync.dma_start(val_pool[0][:], vals_dealt[:, 0, :])
-            nc.sync.dma_start(reserve_cols[:], reserve.rearrange("(b p) o -> p (b o)", p=P))
-        nc.sync.dma_start(val_pool[1][:], vals_dealt[:, 1, :])
-        nc.sync.dma_start(factor_cols[:], slot_factor.rearrange("o (p t) -> p (o t)", t=PACK))
-        for j in range(2, PACK):
+        for j in range(PACK):
             nc.sync.dma_start(val_pool[j][:], vals_dealt[:, j, :])
+        th_cols = sbuf("th_cols", [P, BLOCKS], F32)
+        reserve_cols = sbuf("reserve_cols", [P, BLOCKS], F32)
+        factor_cols = sbuf("factor_cols", [P, PACK], F32)
+        with nc.allow_non_contiguous_dma(reason="one value a partition and row block"):
+            nc.gpsimd.dma_start(th_cols[:], th.rearrange("(b p) o -> p (b o)", p=P))
+            nc.gpsimd.dma_start(reserve_cols[:], reserve.rearrange("(b p) o -> p (b o)", p=P))
+        nc.gpsimd.dma_start(factor_cols[:], slot_factor.rearrange("o (p t) -> p (o t)", t=PACK))
 
         def round_and_interleave(name, raw):
             grouped = sbuf(name, [P, raw.shape[2], PACK], BF16)
@@ -141,6 +139,8 @@ def tile_attend_ttsoftthreshold_pl_kernel(
         second = per_block("second", [P, PACK, P], F32)
 
         a = [scores(codes[:], scales[:], "score") for codes, scales in query_mx]
+        dquery_codes, dquery_scales = quantise("dquery", dquery_grouped, placed(7, 1024, "dquery_codes", [P, Q], U32))
+        ta = [scores(dquery_codes[:, cols(b)], dquery_scales[:, cols(b)], "dscore") for b in range(BLOCKS)]
         for b in range(BLOCKS):
             nc.vector.scalar_tensor_tensor(
                 x[b][:], a[b], th_cols[:, b : b + 1], floor[:].unsqueeze(1).to_broadcast([P, PACK, P]),
@@ -149,13 +149,11 @@ def tile_attend_ttsoftthreshold_pl_kernel(
             nc.scalar.activation(sig[b][:], x[b][:], ACT.Sigmoid)
             nc.gpsimd.tensor_tensor(x_sum_reserve[b][:], x_sum[b][:], reserve_cols[:, b : b + 1], ALU.add)
 
-        dquery_codes, dquery_scales = quantise("dquery", dquery_grouped, placed(7, 1024, "dquery_codes", [P, Q], U32))
-        ta = [scores(dquery_codes[:, cols(b)], dquery_scales[:, cols(b)], "dscore") for b in range(BLOCKS)]
 
         def gather_values(picked, j):
             nc.vector.tensor_copy(picked[:], val_pool[j][:].indirect(offsets[:]))
             words = picked[:].bitcast(F32)
-            turned = psum.tile([P, 2, P], F32, name="turned", tag="turned", bufs=4)
+            turned = psum.tile([P, 2, P], F32, name="turned", tag="turned", bufs=3)
             for u in range(2):
                 nc.tensor.transpose(turned[:, u, :], words[:, u::2], identity[:])
             return turned
@@ -163,24 +161,23 @@ def tile_attend_ttsoftthreshold_pl_kernel(
         def group_values(grouped, turned):
             nc.scalar.copy(grouped[:].bitcast(F32), turned[:].rearrange("p u m -> p m u"))
 
-        turned0 = gather_values(placed(7, 0, "picked0", [P, I], BF16), 0)
-        for b in range(BLOCKS):
-            nc.vector.tensor_tensor(tp[b][:], ta[b], sig[b][:], ALU.mult)
         for b in range(BLOCKS):
             nc.scalar.activation(log_sig[b][:], sig[b][:], ACT.Ln, accum_out=log_sig_sum[b][:])
             nc.scalar.activation(
                 denom[b][:], log_sig_sum[b][:], ACT.Identity, bias=x_sum_reserve[b][:], scale=-1.0
             )
             nc.gpsimd.tensor_tensor(neg_part[b][:], log_sig[b][:], x[b][:], ALU.subtract)
-
-        val_grouped0 = placed(PACK, 2048, "val_grouped0", [P, P, PACK], BF16)
-        group_values(val_grouped0, turned0)
-        turned1 = gather_values(placed(7, 1024, "picked1", [P, I], BF16), 1)
-        inv_denom = [placed(1, 64 * b, "inv_denom%d" % b, [P, 1], F32) for b in range(BLOCKS)]
+        turned = []
+        inv_denom = []
         for b in range(BLOCKS):
+            if b == 0:
+                turned.append(gather_values(placed(7, 0, "picked0", [P, I], BF16), 0))
+            nc.vector.tensor_tensor(tp[b][:], ta[b], sig[b][:], ALU.mult)
+            if b == 0:
+                turned.append(gather_values(placed(7, 1024, "picked1", [P, I], BF16), 1))
+            inv_denom.append(placed(1, 64 * b, "inv_denom%d" % b, [P, 1], F32))
             nc.vector.reciprocal(inv_denom[b][:], denom[b][:])
-        val0_mx = quantise("val0", val_grouped0, placed(7, 2048, "val0_codes", [P, P], U32))
-        turned2 = gather_values(placed(7, 3072, "picked2", [P, I], BF16), 2)
+        turned.append(gather_values(placed(7, 3072, "picked2", [P, I], BF16), 2))
 
         weights_turned = []
         for b in range(BLOCKS):
@@ -196,7 +193,8 @@ def tile_attend_ttsoftthreshold_pl_kernel(
                 )
             weights_turned.append(bank)
 
-        def weigh(grouped, b):
+        def weigh(b):
+            grouped = placed(3, 0, "weights_grouped%d" % b, [P, P, PACK], BF16)
             nc.vector.tensor_tensor(
                 grouped[:],
                 weights_turned[b][:].rearrange("s r q -> s q r"),
@@ -205,45 +203,40 @@ def tile_attend_ttsoftthreshold_pl_kernel(
             )
             return grouped
 
-        middle_grouped = placed(PACK, 4096 + 2048, "middle_grouped", [P, 2 * P, PACK], BF16)
-        group_values(middle_grouped[:, cols(0), :], turned1)
-        group_values(middle_grouped[:, cols(1), :], turned2)
-        weights_grouped0 = weigh(placed(7, 4096, "weights_grouped0", [P, P, PACK], BF16), 0)
-        weights_mx = [quantise("weights0", weights_grouped0, sbuf("weights0_codes", [P, P], U32))]
-        val_grouped3 = sbuf("val_grouped3", [P, P, PACK], BF16)
-        group_values(val_grouped3, gather_values(placed(7, 4096, "picked3", [P, I], BF16), 3))
-        weights_grouped1 = weigh(placed(3, 0, "weights_grouped1", [P, P, PACK], BF16), 1)
-        middle_codes, middle_scales = quantise("middle", middle_grouped, placed(3, 1024, "middle_codes", [P, 2 * P], U32))
-        weights_mx.append(quantise("weights1", weights_grouped1, sbuf("weights1_codes", [P, P], U32)))
-        val_mx = [val0_mx] + [(middle_codes[:, cols(j)], middle_scales[:, cols(j)]) for j in range(2)]
+        val_grouped = placed(PACK, 4096, "val_grouped", [P, PACK * P, PACK], BF16)
+        group_values(val_grouped[:, cols(0), :], turned[0])
+        turned.append(gather_values(placed(2, 0, "picked3", [P, I], BF16), 3))
+        for j in range(1, PACK):
+            group_values(val_grouped[:, cols(j), :], turned[j])
 
-        result = [psum.tile([P, PACK, P], F32, name="result", tag="dscore") for b in range(BLOCKS)]
+        def quantise_values(half):
+            codes, scales = quantise(
+                "val%d" % half, val_grouped[:, 2 * half * P : 2 * (half + 1) * P, :], sbuf("val_codes%d" % half, [P, 2 * P], U32)
+            )
+            return [(codes[:, cols(j)], scales[:, cols(j)]) for j in range(2)]
+
+        weights_mx = [quantise("weights0", weigh(0), sbuf("weights0_codes", [P, P], U32))]
+        val_mx = quantise_values(0)
+        weights_grouped1 = weigh(1)
+        val_mx.extend(quantise_values(1))
+        weights_mx.append(quantise("weights1", weights_grouped1, sbuf("weights1_codes", [P, P], U32)))
+
         staged = per_block("staged", [P, PACK, P], F32)
         out_dealt = out_0.rearrange("(m j) q -> m j q", j=PACK)
-
-        def product(j, b):
-            nc.tensor.matmul_mx(
-                result[b][:, j, :],
-                lhsT=val_mx[j][0][:].bitcast(FP8X4),
-                lhsT_scale=val_mx[j][1][:],
-                rhs=weights_mx[b][0][:].bitcast(FP8X4),
-                rhs_scale=weights_mx[b][1][:],
-                start=True,
-                stop=True,
-            )
-
-        last = PACK - 1
         for b in range(BLOCKS):
-            for j in range(last):
-                product(j, b)
-        nc.scalar.copy(staged[0][:, :last, :], result[0][:, :last, :])
-        val_mx.append(quantise("val3", val_grouped3, sbuf("val3_codes", [P, P], U32)))
-        product(last, 1)
-        product(last, 0)
-        nc.scalar.copy(staged[1][:], result[1][:])
-        nc.vector.tensor_copy(staged[0][:, last, :], result[0][:, last, :])
-        nc.sync.dma_start(out_dealt[:, :, cols(0)], staged[0][:])
-        nc.scalar.dma_start(out_dealt[:, :, cols(1)], staged[1][:])
+            result = psum.tile([P, PACK, P], F32, name="result", tag="dscore")
+            for j in range(PACK):
+                nc.tensor.matmul_mx(
+                    result[:, j, :],
+                    lhsT=val_mx[j][0][:].bitcast(FP8X4),
+                    lhsT_scale=val_mx[j][1][:],
+                    rhs=weights_mx[b][0][:].bitcast(FP8X4),
+                    rhs_scale=weights_mx[b][1][:],
+                    start=True,
+                    stop=True,
+                )
+            nc.scalar.copy(staged[b][:], result[:])
+            nc.sync.dma_start(out_dealt[:, :, cols(b)], staged[b][:])
 
         out_codes = sbuf("out_codes", [P, Q], U32)
         out_scales = sbuf("out_scales", [P, Q], U8)
@@ -253,7 +246,6 @@ def tile_attend_ttsoftthreshold_pl_kernel(
                 out_grouped[b][:].rearrange("m (c i) j -> m c j i", i=4),
                 staged[b][:].rearrange("m j (c i) -> m c j i", i=4),
             )
-        for b in range(BLOCKS):
             nc.vector.quantize_mx(
                 out_codes[:, cols(b)].bitcast(FP8X4),
                 out_scales[:, cols(b)],

@@ -20,7 +20,7 @@ P = 128
 PACK = 4
 BLOCKS = Q // P
 QUADRANTS = 4
-FLOOR = -40.0
+LOG_GUARD = 2.0 ** -63
 POOL_BYTES = T * 4
 
 
@@ -63,10 +63,10 @@ def tile_attend_ttsoftthreshold_pl_kernel(
             out=identity[:], in_=zeros[:, :P], compare_op=ALU.not_equal, fill=1.0, base=0,
             pattern=[[-1, P]], channel_multiplier=1,
         )
-        floor = placed(7, 0, "floor", [P, 1], F32)
-        nc.vector.memset(floor[:], FLOOR)
+        warm_in = sbuf("warm_in", [P, 1], F32)
+        nc.vector.memset(warm_in[:], 0.0)
         warm = sbuf("warm", [P, 1], F32)
-        nc.scalar.activation(warm[:], floor[:], ACT.Sigmoid)
+        nc.scalar.activation(warm[:], warm_in[:], ACT.Sigmoid)
 
         query_raw = placed(5, 4096, "query_raw", [P, PACK, Q], F32)
         nc.sync.dma_start(query_raw[:], query.rearrange("(p t) q -> p t q", t=PACK))
@@ -74,42 +74,42 @@ def tile_attend_ttsoftthreshold_pl_kernel(
         nc.sync.dma_start(dquery_raw[:], dquery.rearrange("(p t) q -> p t q", t=PACK))
         val_pool = [placed(j, 0, "val_pool%d" % j, [P, T], F32) for j in range(PACK)]
         vals_dealt = vals.rearrange("(m j) t -> m j t", j=PACK)
-        for j in range(PACK):
-            nc.sync.dma_start(val_pool[j][:], vals_dealt[:, j, :])
-        th_cols = sbuf("th_cols", [P, BLOCKS], F32)
-        reserve_cols = sbuf("reserve_cols", [P, BLOCKS], F32)
-        factor_cols = sbuf("factor_cols", [P, PACK], F32)
+        th_cols = placed(6, 0, "th_cols", [P, BLOCKS], F32)
+        reserve_cols = placed(6, 64, "reserve_cols", [P, BLOCKS], F32)
+        factor_cols = placed(6, 128, "factor_cols", [P, PACK], F32)
         with nc.allow_non_contiguous_dma(reason="one value a partition and row block"):
-            nc.gpsimd.dma_start(th_cols[:], th.rearrange("(b p) o -> p (b o)", p=P))
-            nc.gpsimd.dma_start(reserve_cols[:], reserve.rearrange("(b p) o -> p (b o)", p=P))
-        nc.gpsimd.dma_start(factor_cols[:], slot_factor.rearrange("o (p t) -> p (o t)", t=PACK))
+            nc.sync.dma_start(th_cols[:], th.rearrange("(b p) o -> p (b o)", p=P))
+            nc.sync.dma_start(val_pool[0][:], vals_dealt[:, 0, :])
+            nc.sync.dma_start(val_pool[1][:], vals_dealt[:, 1, :])
+            nc.sync.dma_start(reserve_cols[:], reserve.rearrange("(b p) o -> p (b o)", p=P))
+        nc.sync.dma_start(factor_cols[:], slot_factor.rearrange("o (p t) -> p (o t)", t=PACK))
+        for j in range(2, PACK):
+            nc.sync.dma_start(val_pool[j][:], vals_dealt[:, j, :])
 
-        def round_and_interleave(name, raw):
-            grouped = sbuf(name, [P, raw.shape[2], PACK], BF16)
-            nc.scalar.copy(
-                grouped[:].rearrange("p (c i) t -> p c t i", i=4),
-                raw.rearrange("p t (c i) -> p c t i", i=4),
-            )
-            return grouped
+        def round_and_interleave(copy, grouped, raw):
+            copy(grouped.rearrange("p (c i) t -> p c t i", i=4), raw.rearrange("p t (c i) -> p c t i", i=4))
 
-        def quantise(name, grouped, codes):
-            scales = sbuf(name + "_scales", [P, codes.shape[1]], U8)
-            nc.vector.quantize_mx(codes[:].bitcast(FP8X4), scales[:], grouped[:].rearrange("p c t -> p (c t)"))
-            return codes, scales
+        def negate(out, in_):
+            nc.scalar.activation(out, in_, ACT.Copy, scale=-1.0)
+
+        def quantise(codes, scales, grouped):
+            nc.vector.quantize_mx(codes.bitcast(FP8X4), scales, grouped.rearrange("p c t -> p (c t)"))
 
         key_words = sbuf("key_words", [P, I], U16)
         nc.vector.tensor_copy(key_words[:], key_word_pool[:].indirect(offsets[:]))
         key_scales = sbuf("key_scales", [P, I], U8)
         nc.vector.tensor_copy(key_scales[:], key_scale_pool[:].indirect(offsets[:]))
-        query_mx = [
-            quantise(
-                "query%d" % b,
-                round_and_interleave("query_grouped%d" % b, query_raw[:, :, cols(b)]),
-                sbuf("query_codes%d" % b, [P, P], U32),
-            )
-            for b in range(BLOCKS)
-        ]
-        dquery_grouped = round_and_interleave("dquery_grouped", dquery_raw[:])
+        query_grouped = sbuf("query_grouped", [P, Q, PACK], BF16)
+        query_codes = sbuf("query_codes", [P, Q], U32)
+        query_scales = sbuf("query_scales", [P, Q], U8)
+        for b in range(BLOCKS):
+            round_and_interleave(negate, query_grouped[:, cols(b), :], query_raw[:, :, cols(b)])
+            quantise(query_codes[:, cols(b)], query_scales[:, cols(b)], query_grouped[:, cols(b), :])
+        dquery_grouped = placed(7, 0, "dquery_grouped", [P, Q, PACK], BF16)
+        round_and_interleave(nc.scalar.copy, dquery_grouped[:], dquery_raw[:])
+        dquery_codes = sbuf("dquery_codes", [P, Q], U32)
+        dquery_scales = sbuf("dquery_scales", [P, Q], U8)
+        quantise(dquery_codes[:], dquery_scales[:], dquery_grouped[:])
 
         def scores(codes, scales, tag):
             bank = psum.tile([P, I], F32, name=tag, tag=tag)
@@ -122,135 +122,136 @@ def tile_attend_ttsoftthreshold_pl_kernel(
                 start=True,
                 stop=True,
             )
-            return bank[:].rearrange("q (s r) -> q r s", r=PACK)
+            return bank
 
-        x = per_block("x", [P, PACK, P], F32)
-        x_sum = per_block("x_sum", [P, 1], F32)
-        x_sum_reserve = per_block("x_sum_reserve", [P, 1], F32)
-        sig = [placed(5, 0, "sig0", [P, PACK, P], F32), placed(PACK, 2048, "sig1", [P, PACK, P], F32)]
-        log_sig = per_block("log_sig", [P, PACK, P], F32)
-        log_sig_sum = per_block("log_sig_sum", [P, 1], F32)
-        denom = [placed(7, 2048 + 1024 * b, "denom%d" % b, [P, 1], F32) for b in range(BLOCKS)]
-        neg_part = [placed(PACK, 4096 + 2048 * b, "neg_part%d" % b, [P, PACK, P], F32) for b in range(BLOCKS)]
-        tp = per_block("tp", [P, PACK, P], F32)
-        first_sum = per_block("first_sum", [P, 1], F32)
-        first = per_block("first", [P, PACK, P], F32)
-        second_scale = per_block("second_scale", [P, 1], F32)
-        second = per_block("second", [P, PACK, P], F32)
-
-        a = [scores(codes[:], scales[:], "score") for codes, scales in query_mx]
-        dquery_codes, dquery_scales = quantise("dquery", dquery_grouped, placed(7, 1024, "dquery_codes", [P, Q], U32))
+        a = [scores(query_codes[:, cols(b)], query_scales[:, cols(b)], "score") for b in range(BLOCKS)]
         ta = [scores(dquery_codes[:, cols(b)], dquery_scales[:, cols(b)], "dscore") for b in range(BLOCKS)]
+
+        neg_th = [placed(8, 2048 * (1 - b), "neg_th%d" % b, [P, 1], F32) for b in range(BLOCKS)]
+        co_sig = [placed(5, 0, "co_sig0", [P, I], F32), placed(PACK, 0, "co_sig1", [P, I], F32)]
+        sig = [placed(7, 2048 * (b + 1), "sig%d" % b, [P, I], F32) for b in range(BLOCKS)]
         for b in range(BLOCKS):
-            nc.vector.scalar_tensor_tensor(
-                x[b][:], a[b], th_cols[:, b : b + 1], floor[:].unsqueeze(1).to_broadcast([P, PACK, P]),
-                ALU.subtract, ALU.max, accum_out=x_sum[b][:],
-            )
-            nc.scalar.activation(sig[b][:], x[b][:], ACT.Sigmoid)
-            nc.gpsimd.tensor_tensor(x_sum_reserve[b][:], x_sum[b][:], reserve_cols[:, b : b + 1], ALU.add)
+            nc.gpsimd.tensor_scalar(neg_th[b][:], th_cols[:, b : b + 1], -1.0, 0.0, ALU.mult, ALU.add)
+            nc.scalar.activation(co_sig[b][:], a[b][:], ACT.Sigmoid, bias=th_cols[:, b : b + 1])
+        for b in range(BLOCKS):
+            nc.scalar.activation(sig[b][:], a[b][:], ACT.Sigmoid, bias=neg_th[b][:], scale=-1.0)
+        log_co_sig = [placed(8, 4096 * b, "log_co_sig%d" % b, [P, I], F32) for b in range(BLOCKS)]
+        for b in range(BLOCKS):
+            nc.scalar.activation(log_co_sig[b][:], co_sig[b][:], ACT.Ln, bias=LOG_GUARD)
+        tp_sum = per_block("tp_sum", [P, 1], F32)
+        neg_part_sum = per_block("neg_part_sum", [P, 1], F32)
+        denom = per_block("denom", [P, 1], F32)
+        share = per_block("share", [P, 1], F32)
 
-
-        def gather_values(picked, j):
-            nc.vector.tensor_copy(picked[:], val_pool[j][:].indirect(offsets[:]))
-            words = picked[:].bitcast(F32)
-            turned = psum.tile([P, 2, P], F32, name="turned", tag="turned", bufs=3)
+        def turn(rows):
+            words = rows[:].bitcast(F32)
+            turned = psum.tile([P, 2, P], F32, name="turned", tag="turned", bufs=4)
             for u in range(2):
                 nc.tensor.transpose(turned[:, u, :], words[:, u::2], identity[:])
             return turned
 
-        def group_values(grouped, turned):
-            nc.scalar.copy(grouped[:].bitcast(F32), turned[:].rearrange("p u m -> p m u"))
+        def gather_values(picked, j):
+            nc.vector.tensor_copy(picked[:], val_pool[j][:].indirect(offsets[:]))
+            return turn(picked)
 
+        def group(grouped, turned):
+            nc.scalar.copy(grouped.bitcast(F32), turned[:].rearrange("p u m -> p m u"))
+
+        val_turned = [gather_values(placed(7, 0, "picked0", [P, I], BF16), 0)]
+        tp = [placed(0, 2048 * b, "tp%d" % b, [P, I], F32) for b in range(BLOCKS)]
         for b in range(BLOCKS):
-            nc.scalar.activation(log_sig[b][:], sig[b][:], ACT.Ln, accum_out=log_sig_sum[b][:])
-            nc.scalar.activation(
-                denom[b][:], log_sig_sum[b][:], ACT.Identity, bias=x_sum_reserve[b][:], scale=-1.0
+            nc.vector.scalar_tensor_tensor(
+                tp[b][:], ta[b][:], 1.0, sig[b][:], ALU.mult, ALU.mult, accum_out=tp_sum[b][:]
             )
-            nc.gpsimd.tensor_tensor(neg_part[b][:], log_sig[b][:], x[b][:], ALU.subtract)
-        turned = []
-        inv_denom = []
-        for b in range(BLOCKS):
-            if b == 0:
-                turned.append(gather_values(placed(7, 0, "picked0", [P, I], BF16), 0))
-            nc.vector.tensor_tensor(tp[b][:], ta[b], sig[b][:], ALU.mult)
-            if b == 0:
-                turned.append(gather_values(placed(7, 1024, "picked1", [P, I], BF16), 1))
-            inv_denom.append(placed(1, 64 * b, "inv_denom%d" % b, [P, 1], F32))
-            nc.vector.reciprocal(inv_denom[b][:], denom[b][:])
-        turned.append(gather_values(placed(7, 3072, "picked2", [P, I], BF16), 2))
+        factor_rows = psum.tile([P, PACK, P], F32, name="factor_rows", tag="dscore")
+        for t in range(PACK):
+            nc.tensor.transpose(factor_rows[:, t, :], factor_cols[:, t : t + 1].to_broadcast([P, P]), identity[:])
+        val_turned.append(gather_values(placed(7, 2048, "picked1", [P, I], BF16), 1))
+        val_grouped = placed(PACK, 0, "val_grouped", [P, PACK * P, PACK], BF16)
+        for j in range(2):
+            group(val_grouped[:, cols(j), :], val_turned[j])
 
-        weights_turned = []
+        neg_part = [placed(1, 2048 * b, "neg_part%d" % b, [P, I], F32) for b in range(BLOCKS)]
         for b in range(BLOCKS):
-            nc.scalar.activation(first[b][:], tp[b][:], ACT.Copy, scale=inv_denom[b][:], accum_out=first_sum[b][:])
-            nc.scalar.activation(second_scale[b][:], first_sum[b][:], ACT.Copy, scale=inv_denom[b][:])
-            nc.scalar.activation(second[b][:], neg_part[b][:], ACT.Copy, scale=second_scale[b][:])
-            bank = psum.tile([P, PACK, P], F32, name="score", tag="score")
-            terms = [(term, r) for term in (first[b], second[b]) for r in range(PACK)]
-            for n, (term, r) in enumerate(terms):
-                nc.tensor.matmul(
-                    bank[:, r, :], term[:, r, :], identity[:],
-                    start=(n == 0), stop=(n == len(terms) - 1), is_transpose=True,
-                )
-            weights_turned.append(bank)
+            nc.vector.scalar_tensor_tensor(
+                neg_part[b][:], a[b][:], th_cols[:, b : b + 1], log_co_sig[b][:], ALU.add, ALU.min,
+                accum_out=neg_part_sum[b][:],
+            )
+            nc.gpsimd.tensor_scalar(
+                denom[b][:], neg_part_sum[b][:], -1.0, reserve_cols[:, b : b + 1], ALU.mult, ALU.add
+            )
 
-        def weigh(b):
-            grouped = placed(3, 0, "weights_grouped%d" % b, [P, P, PACK], BF16)
-            nc.vector.tensor_tensor(
-                grouped[:],
-                weights_turned[b][:].rearrange("s r q -> s q r"),
-                factor_cols[:].unsqueeze(1).to_broadcast([P, P, PACK]),
+        def normalise(inv, b):
+            nc.vector.reciprocal(inv[:], denom[b][:])
+            nc.gpsimd.tensor_scalar(share[b][:], tp_sum[b][:], inv[:], 0.0, ALU.mult, ALU.add)
+            return inv
+
+        inv_denom = [normalise(sbuf("inv_denom0", [P, 1], F32), 0)]
+        val_turned.append(gather_values(placed(8, 4096, "picked2", [P, I], BF16), 2))
+        group(val_grouped[:, cols(2), :], val_turned[2])
+        inv_denom.append(normalise(placed(2, 0, "inv_denom1", [P, 1], F32), 1))
+
+        numerator = [placed(2, 2048 * (b + 1), "numerator%d" % b, [P, I], F32) for b in range(BLOCKS)]
+        for b in range(BLOCKS):
+            nc.vector.scalar_tensor_tensor(numerator[b][:], neg_part[b][:], share[b][:], tp[b][:], ALU.mult, ALU.add)
+        weights_grouped = sbuf("weights_grouped", [P, Q, PACK], BF16)
+        for b in range(BLOCKS):
+            weights = sbuf("weights%d" % b, [P, I], BF16)
+            nc.vector.scalar_tensor_tensor(
+                weights[:].rearrange("q (s t) -> q s t", t=PACK),
+                numerator[b][:].rearrange("q (s t) -> q s t", t=PACK),
+                inv_denom[b][:],
+                factor_rows[:].rearrange("q t s -> q s t"),
+                ALU.mult,
                 ALU.mult,
             )
-            return grouped
+            group(weights_grouped[:, cols(b), :], turn(weights))
+        last = PACK - 1
+        group(val_grouped[:, cols(last), :], gather_values(placed(2, 4096, "picked3", [P, I], BF16), last))
 
-        val_grouped = placed(PACK, 4096, "val_grouped", [P, PACK * P, PACK], BF16)
-        group_values(val_grouped[:, cols(0), :], turned[0])
-        turned.append(gather_values(placed(2, 0, "picked3", [P, I], BF16), 3))
-        for j in range(1, PACK):
-            group_values(val_grouped[:, cols(j), :], turned[j])
+        val_codes = placed(3, 0, "val_codes", [P, PACK * P], U32)
+        val_scales = sbuf("val_scales", [P, PACK * P], U8)
+        weights_codes = placed(3, 2048, "weights_codes", [P, Q], U32)
+        weights_scales = sbuf("weights_scales", [P, Q], U8)
 
-        def quantise_values(half):
-            codes, scales = quantise(
-                "val%d" % half, val_grouped[:, 2 * half * P : 2 * (half + 1) * P, :], sbuf("val_codes%d" % half, [P, 2 * P], U32)
-            )
-            return [(codes[:, cols(j)], scales[:, cols(j)]) for j in range(2)]
+        def quantise_values(part):
+            quantise(val_codes[:, part], val_scales[:, part], val_grouped[:, part, :])
 
-        weights_mx = [quantise("weights0", weigh(0), sbuf("weights0_codes", [P, P], U32))]
-        val_mx = quantise_values(0)
-        weights_grouped1 = weigh(1)
-        val_mx.extend(quantise_values(1))
-        weights_mx.append(quantise("weights1", weights_grouped1, sbuf("weights1_codes", [P, P], U32)))
+        quantise_values(slice(0, 2 * P))
+        quantise_values(cols(2))
+        quantise(weights_codes[:], weights_scales[:], weights_grouped[:])
+        quantise_values(cols(last))
 
-        staged = per_block("staged", [P, PACK, P], F32)
+        staged = sbuf("staged", [P, PACK, Q], F32)
         out_dealt = out_0.rearrange("(m j) q -> m j q", j=PACK)
-        for b in range(BLOCKS):
-            result = psum.tile([P, PACK, P], F32, name="result", tag="dscore")
-            for j in range(PACK):
+
+        def product(planes, tag, copy):
+            result = psum.tile([P, len(planes), Q], F32, name="result", tag=tag)
+            for n, j in enumerate(planes):
                 nc.tensor.matmul_mx(
-                    result[:, j, :],
-                    lhsT=val_mx[j][0][:].bitcast(FP8X4),
-                    lhsT_scale=val_mx[j][1][:],
-                    rhs=weights_mx[b][0][:].bitcast(FP8X4),
-                    rhs_scale=weights_mx[b][1][:],
+                    result[:, n, :],
+                    lhsT=val_codes[:, cols(j)].bitcast(FP8X4),
+                    lhsT_scale=val_scales[:, cols(j)],
+                    rhs=weights_codes[:].bitcast(FP8X4),
+                    rhs_scale=weights_scales[:],
                     start=True,
                     stop=True,
                 )
-            nc.scalar.copy(staged[b][:], result[:])
-            nc.sync.dma_start(out_dealt[:, :, cols(b)], staged[b][:])
+            copy(staged[:, planes.start : planes.stop, :], result[:])
 
+        product(range(0, 2), "score", nc.scalar.copy)
+        product(range(2, last), "score", nc.scalar.copy)
+        nc.sync.dma_start(out_dealt[:, :last, :], staged[:, :last, :])
+        product(range(last, PACK), "dscore", nc.vector.tensor_copy)
+        nc.sync.dma_start(out_dealt[:, last, :], staged[:, last, :])
+
+        out_grouped = sbuf("out_grouped", [P, Q, PACK], BF16)
         out_codes = sbuf("out_codes", [P, Q], U32)
         out_scales = sbuf("out_scales", [P, Q], U8)
-        out_grouped = per_block("out_grouped", [P, P, PACK], BF16)
+        for b, copy in enumerate((nc.vector.tensor_copy, nc.scalar.copy)):
+            round_and_interleave(copy, out_grouped[:, cols(b), :], staged[:, :, cols(b)])
         for b in range(BLOCKS):
-            nc.vector.tensor_copy(
-                out_grouped[b][:].rearrange("m (c i) j -> m c j i", i=4),
-                staged[b][:].rearrange("m j (c i) -> m c j i", i=4),
-            )
-            nc.vector.quantize_mx(
-                out_codes[:, cols(b)].bitcast(FP8X4),
-                out_scales[:, cols(b)],
-                out_grouped[b][:].rearrange("m q j -> m (q j)"),
-            )
+            quantise(out_codes[:, cols(b)], out_scales[:, cols(b)], out_grouped[:, cols(b), :])
         nc.sync.dma_start(out_1[0].rearrange("p c t -> p (c t)").bitcast(I32), out_codes[:].bitcast(I32))
         for quad in range(QUADRANTS):
             queue = nc.sync if quad % 2 == 0 else nc.scalar

@@ -20,7 +20,7 @@ P = 128
 PACK = 4
 BLOCKS = Q // P
 QUADRANTS = 4
-LOG_GUARD = 2.0 ** -63
+FLOOR = -40.0
 POOL_BYTES = T * 4
 
 
@@ -63,10 +63,9 @@ def tile_attend_ttsoftthreshold_pl_kernel(
             out=identity[:], in_=zeros[:, :P], compare_op=ALU.not_equal, fill=1.0, base=0,
             pattern=[[-1, P]], channel_multiplier=1,
         )
-        warm_in = sbuf("warm_in", [P, 1], F32)
-        nc.vector.memset(warm_in[:], 0.0)
-        warm = sbuf("warm", [P, 1], F32)
-        nc.scalar.activation(warm[:], warm_in[:], ACT.Sigmoid)
+        floor = [placed(7, 1024 * b, "floor%d" % b, [P, 1], F32) for b in range(BLOCKS)]
+        for b in range(BLOCKS):
+            nc.vector.memset(floor[b][:], FLOOR)
 
         query_raw = placed(5, 4096, "query_raw", [P, PACK, Q], F32)
         nc.sync.dma_start(query_raw[:], query.rearrange("(p t) q -> p t q", t=PACK))
@@ -74,11 +73,11 @@ def tile_attend_ttsoftthreshold_pl_kernel(
         nc.sync.dma_start(dquery_raw[:], dquery.rearrange("(p t) q -> p t q", t=PACK))
         val_pool = [placed(j, 0, "val_pool%d" % j, [P, T], F32) for j in range(PACK)]
         vals_dealt = vals.rearrange("(m j) t -> m j t", j=PACK)
-        th_cols = placed(6, 0, "th_cols", [P, BLOCKS], F32)
+        th_cols = sbuf("th_cols", [P, BLOCKS], F32)
         reserve_cols = placed(6, 64, "reserve_cols", [P, BLOCKS], F32)
         factor_cols = placed(6, 128, "factor_cols", [P, PACK], F32)
         with nc.allow_non_contiguous_dma(reason="one value a partition and row block"):
-            nc.sync.dma_start(th_cols[:], th.rearrange("(b p) o -> p (b o)", p=P))
+            nc.gpsimd.dma_start(th_cols[:], th.rearrange("(b p) o -> p (b o)", p=P))
             nc.sync.dma_start(val_pool[0][:], vals_dealt[:, 0, :])
             nc.sync.dma_start(val_pool[1][:], vals_dealt[:, 1, :])
             nc.sync.dma_start(reserve_cols[:], reserve.rearrange("(b p) o -> p (b o)", p=P))
@@ -89,9 +88,6 @@ def tile_attend_ttsoftthreshold_pl_kernel(
         def round_and_interleave(copy, grouped, raw):
             copy(grouped.rearrange("p (c i) t -> p c t i", i=4), raw.rearrange("p t (c i) -> p c t i", i=4))
 
-        def negate(out, in_):
-            nc.scalar.activation(out, in_, ACT.Copy, scale=-1.0)
-
         def quantise(codes, scales, grouped):
             nc.vector.quantize_mx(codes.bitcast(FP8X4), scales, grouped.rearrange("p c t -> p (c t)"))
 
@@ -99,17 +95,14 @@ def tile_attend_ttsoftthreshold_pl_kernel(
         nc.vector.tensor_copy(key_words[:], key_word_pool[:].indirect(offsets[:]))
         key_scales = sbuf("key_scales", [P, I], U8)
         nc.vector.tensor_copy(key_scales[:], key_scale_pool[:].indirect(offsets[:]))
-        query_grouped = sbuf("query_grouped", [P, Q, PACK], BF16)
+        query_grouped = placed(8, 0, "query_grouped", [P, Q, PACK], BF16)
         query_codes = sbuf("query_codes", [P, Q], U32)
         query_scales = sbuf("query_scales", [P, Q], U8)
         for b in range(BLOCKS):
-            round_and_interleave(negate, query_grouped[:, cols(b), :], query_raw[:, :, cols(b)])
+            round_and_interleave(nc.scalar.copy, query_grouped[:, cols(b), :], query_raw[:, :, cols(b)])
             quantise(query_codes[:, cols(b)], query_scales[:, cols(b)], query_grouped[:, cols(b), :])
-        dquery_grouped = placed(7, 0, "dquery_grouped", [P, Q, PACK], BF16)
-        round_and_interleave(nc.scalar.copy, dquery_grouped[:], dquery_raw[:])
-        dquery_codes = sbuf("dquery_codes", [P, Q], U32)
-        dquery_scales = sbuf("dquery_scales", [P, Q], U8)
-        quantise(dquery_codes[:], dquery_scales[:], dquery_grouped[:])
+        dquery_grouped = placed(8, 0, "dquery_grouped", [P, Q, PACK], BF16)
+        round_and_interleave(nc.vector.tensor_copy, dquery_grouped[:], dquery_raw[:])
 
         def scores(codes, scales, tag):
             bank = psum.tile([P, I], F32, name=tag, tag=tag)
@@ -125,23 +118,35 @@ def tile_attend_ttsoftthreshold_pl_kernel(
             return bank
 
         a = [scores(query_codes[:, cols(b)], query_scales[:, cols(b)], "score") for b in range(BLOCKS)]
-        ta = [scores(dquery_codes[:, cols(b)], dquery_scales[:, cols(b)], "dscore") for b in range(BLOCKS)]
 
-        neg_th = [placed(8, 2048 * (1 - b), "neg_th%d" % b, [P, 1], F32) for b in range(BLOCKS)]
-        co_sig = [placed(5, 0, "co_sig0", [P, I], F32), placed(PACK, 0, "co_sig1", [P, I], F32)]
-        sig = [placed(7, 2048 * (b + 1), "sig%d" % b, [P, I], F32) for b in range(BLOCKS)]
-        for b in range(BLOCKS):
-            nc.gpsimd.tensor_scalar(neg_th[b][:], th_cols[:, b : b + 1], -1.0, 0.0, ALU.mult, ALU.add)
-            nc.scalar.activation(co_sig[b][:], a[b][:], ACT.Sigmoid, bias=th_cols[:, b : b + 1])
-        for b in range(BLOCKS):
-            nc.scalar.activation(sig[b][:], a[b][:], ACT.Sigmoid, bias=neg_th[b][:], scale=-1.0)
-        log_co_sig = [placed(8, 4096 * b, "log_co_sig%d" % b, [P, I], F32) for b in range(BLOCKS)]
-        for b in range(BLOCKS):
-            nc.scalar.activation(log_co_sig[b][:], co_sig[b][:], ACT.Ln, bias=LOG_GUARD)
-        tp_sum = per_block("tp_sum", [P, 1], F32)
-        neg_part_sum = per_block("neg_part_sum", [P, 1], F32)
+        x = per_block("x", [P, I], F32)
+        x_sum = per_block("x_sum", [P, 1], F32)
+        x_sum_reserve = per_block("x_sum_reserve", [P, 1], F32)
+        sig = [sbuf("sig0", [P, I], F32), placed(PACK, 0, "sig1", [P, I], F32)]
+        log_sig = per_block("log_sig", [P, I], F32)
+        log_sig_sum = per_block("log_sig_sum", [P, 1], F32)
         denom = per_block("denom", [P, 1], F32)
+        neg_part = per_block("neg_part", [P, I], F32)
+        tp_sum = per_block("tp_sum", [P, 1], F32)
         share = per_block("share", [P, 1], F32)
+
+        for b in range(BLOCKS):
+            nc.vector.scalar_tensor_tensor(
+                x[b][:], a[b][:], th_cols[:, b : b + 1], floor[b][:].to_broadcast([P, I]),
+                ALU.subtract, ALU.max, accum_out=x_sum[b][:],
+            )
+            nc.scalar.activation(sig[b][:], x[b][:], ACT.Sigmoid)
+            nc.gpsimd.tensor_tensor(x_sum_reserve[b][:], x_sum[b][:], reserve_cols[:, b : b + 1], ALU.add)
+        dquery_codes = placed(7, 0, "dquery_codes", [P, Q], U32)
+        dquery_scales = sbuf("dquery_scales", [P, Q], U8)
+        quantise(dquery_codes[:], dquery_scales[:], dquery_grouped[:])
+        ta = [scores(dquery_codes[:, cols(b)], dquery_scales[:, cols(b)], "dscore") for b in range(BLOCKS)]
+        for b in range(BLOCKS):
+            nc.scalar.activation(log_sig[b][:], sig[b][:], ACT.Ln, accum_out=log_sig_sum[b][:])
+            nc.scalar.activation(
+                denom[b][:], log_sig_sum[b][:], ACT.Identity, bias=x_sum_reserve[b][:], scale=-1.0
+            )
+            nc.gpsimd.tensor_tensor(neg_part[b][:], log_sig[b][:], x[b][:], ALU.subtract)
 
         def turn(rows):
             words = rows[:].bitcast(F32)
@@ -157,7 +162,7 @@ def tile_attend_ttsoftthreshold_pl_kernel(
         def group(grouped, turned):
             nc.scalar.copy(grouped.bitcast(F32), turned[:].rearrange("p u m -> p m u"))
 
-        val_turned = [gather_values(placed(7, 0, "picked0", [P, I], BF16), 0)]
+        val_turned = [gather_values(sbuf("picked0", [P, I], BF16), 0)]
         tp = [placed(0, 2048 * b, "tp%d" % b, [P, I], F32) for b in range(BLOCKS)]
         for b in range(BLOCKS):
             nc.vector.scalar_tensor_tensor(
@@ -166,32 +171,18 @@ def tile_attend_ttsoftthreshold_pl_kernel(
         factor_rows = psum.tile([P, PACK, P], F32, name="factor_rows", tag="dscore")
         for t in range(PACK):
             nc.tensor.transpose(factor_rows[:, t, :], factor_cols[:, t : t + 1].to_broadcast([P, P]), identity[:])
-        val_turned.append(gather_values(placed(7, 2048, "picked1", [P, I], BF16), 1))
+        val_turned.append(gather_values(sbuf("picked1", [P, I], BF16), 1))
         val_grouped = placed(PACK, 0, "val_grouped", [P, PACK * P, PACK], BF16)
         for j in range(2):
             group(val_grouped[:, cols(j), :], val_turned[j])
-
-        neg_part = [placed(1, 2048 * b, "neg_part%d" % b, [P, I], F32) for b in range(BLOCKS)]
+        inv_denom = [placed(1, 64 * b, "inv_denom%d" % b, [P, 1], F32) for b in range(BLOCKS)]
         for b in range(BLOCKS):
-            nc.vector.scalar_tensor_tensor(
-                neg_part[b][:], a[b][:], th_cols[:, b : b + 1], log_co_sig[b][:], ALU.add, ALU.min,
-                accum_out=neg_part_sum[b][:],
-            )
-            nc.gpsimd.tensor_scalar(
-                denom[b][:], neg_part_sum[b][:], -1.0, reserve_cols[:, b : b + 1], ALU.mult, ALU.add
-            )
-
-        def normalise(inv, b):
-            nc.vector.reciprocal(inv[:], denom[b][:])
-            nc.gpsimd.tensor_scalar(share[b][:], tp_sum[b][:], inv[:], 0.0, ALU.mult, ALU.add)
-            return inv
-
-        inv_denom = [normalise(sbuf("inv_denom0", [P, 1], F32), 0)]
-        val_turned.append(gather_values(placed(8, 4096, "picked2", [P, I], BF16), 2))
+            nc.vector.reciprocal(inv_denom[b][:], denom[b][:])
+            nc.scalar.activation(share[b][:], tp_sum[b][:], ACT.Copy, scale=inv_denom[b][:])
+        val_turned.append(gather_values(sbuf("picked2", [P, I], BF16), 2))
         group(val_grouped[:, cols(2), :], val_turned[2])
-        inv_denom.append(normalise(placed(2, 0, "inv_denom1", [P, 1], F32), 1))
 
-        numerator = [placed(2, 2048 * (b + 1), "numerator%d" % b, [P, I], F32) for b in range(BLOCKS)]
+        numerator = [placed(2, 2048 * b, "numerator%d" % b, [P, I], F32) for b in range(BLOCKS)]
         for b in range(BLOCKS):
             nc.vector.scalar_tensor_tensor(numerator[b][:], neg_part[b][:], share[b][:], tp[b][:], ALU.mult, ALU.add)
         weights_grouped = sbuf("weights_grouped", [P, Q, PACK], BF16)
@@ -207,7 +198,7 @@ def tile_attend_ttsoftthreshold_pl_kernel(
             )
             group(weights_grouped[:, cols(b), :], turn(weights))
         last = PACK - 1
-        group(val_grouped[:, cols(last), :], gather_values(placed(2, 4096, "picked3", [P, I], BF16), last))
+        group(val_grouped[:, cols(last), :], gather_values(placed(2, 0, "picked3", [P, I], BF16), last))
 
         val_codes = placed(3, 0, "val_codes", [P, PACK * P], U32)
         val_scales = sbuf("val_scales", [P, PACK * P], U8)

@@ -20,8 +20,15 @@ P = 128
 PACK = 4
 BLOCKS = Q // P
 QUADRANTS = 4
-FLOOR = -40.0
-POOL_BYTES = T * 4
+QUADRANT_ROWS = P // QUADRANTS
+SCALE_ROWS = 4
+LINE = 4
+GUARD_SCORE = -40.0
+
+REGION_BYTES = T * 4
+ROW_BYTES = I * 4
+ROUNDED, QUERIES, COLUMNS, SIGMOIDS, LOGS, NUMERATORS = range(PACK, PACK + 6)
+SCALAR_PLANE = 2
 
 
 def tile_attend_ttsoftthreshold_pl_kernel(
@@ -37,13 +44,19 @@ def tile_attend_ttsoftthreshold_pl_kernel(
             return held.tile(shape, dtype, name=name, align_bytes=64)
 
         def placed(region, at, name, shape, dtype):
-            return reuse.tile(shape, dtype, name=name, align_bytes=64, offset=region * POOL_BYTES + at)
+            return reuse.tile(shape, dtype, name=name, align_bytes=64, offset=region * REGION_BYTES + at)
 
         def per_block(name, shape, dtype):
             return [sbuf("%s%d" % (name, b), shape, dtype) for b in range(BLOCKS)]
 
-        def cols(b):
-            return slice(b * P, (b + 1) * P)
+        def cols(n):
+            return slice(n * P, (n + 1) * P)
+
+        def live_rows(scale_tile, quad):
+            return scale_tile[QUADRANT_ROWS * quad : QUADRANT_ROWS * quad + SCALE_ROWS, :].bitcast(I32)
+
+        def dram_rows(scale_rows, quad):
+            return scale_rows[0, SCALE_ROWS * quad : SCALE_ROWS * (quad + 1), :].bitcast(I32)
 
         offsets = held.tile([P, I // 16], U16, name="offsets")
         nc.sync.dma_start(offsets[:], offs)
@@ -52,31 +65,30 @@ def tile_attend_ttsoftthreshold_pl_kernel(
         key_scale_pool = sbuf("key_scale_pool", [P, T], U8)
         nc.gpsimd.memset(key_scale_pool[:].bitcast(I32), 0)
         for quad in range(QUADRANTS):
-            nc.sync.dma_start(
-                key_scale_pool[32 * quad : 32 * quad + 4, :].bitcast(I32),
-                keys_scales[0, 4 * quad : 4 * quad + 4, :].bitcast(I32),
-            )
-        zeros = placed(0, 0, "zeros", [P, 7 * T], F32)
+            nc.sync.dma_start(live_rows(key_scale_pool, quad), dram_rows(keys_scales, quad))
+
+        zeros = placed(0, 0, "zeros", [P, (COLUMNS + 1) * T], F32)
         nc.vector.memset(zeros[:, :P], 0.0)
         identity = sbuf("identity", [P, P], F32)
         nc.gpsimd.affine_select(
             out=identity[:], in_=zeros[:, :P], compare_op=ALU.not_equal, fill=1.0, base=0,
             pattern=[[-1, P]], channel_multiplier=1,
         )
-        floor = [placed(7, 1024 * b, "floor%d" % b, [P, 1], F32) for b in range(BLOCKS)]
-        for b in range(BLOCKS):
-            nc.vector.memset(floor[b][:], FLOOR)
+        guard_score = sbuf("guard_score", [P, 1], F32)
+        nc.vector.memset(guard_score[:], GUARD_SCORE)
+        guard = sbuf("guard", [P, 1], F32)
+        nc.scalar.activation(guard[:], guard_score[:], ACT.Sigmoid)
 
-        query_raw = placed(5, 4096, "query_raw", [P, PACK, Q], F32)
+        query_raw = placed(QUERIES, PACK * Q * 4, "query_raw", [P, PACK, Q], F32)
         nc.sync.dma_start(query_raw[:], query.rearrange("(p t) q -> p t q", t=PACK))
-        dquery_raw = placed(5, 0, "dquery_raw", [P, PACK, Q], F32)
+        dquery_raw = placed(QUERIES, 0, "dquery_raw", [P, PACK, Q], F32)
         nc.sync.dma_start(dquery_raw[:], dquery.rearrange("(p t) q -> p t q", t=PACK))
         val_pool = [placed(j, 0, "val_pool%d" % j, [P, T], F32) for j in range(PACK)]
         vals_dealt = vals.rearrange("(m j) t -> m j t", j=PACK)
         th_cols = sbuf("th_cols", [P, BLOCKS], F32)
-        reserve_cols = placed(6, 64, "reserve_cols", [P, BLOCKS], F32)
-        factor_cols = placed(6, 128, "factor_cols", [P, PACK], F32)
-        with nc.allow_non_contiguous_dma(reason="one value a partition and row block"):
+        reserve_cols = placed(COLUMNS, 64, "reserve_cols", [P, BLOCKS], F32)
+        factor_cols = placed(COLUMNS, 128, "factor_cols", [P, PACK], F32)
+        with nc.allow_non_contiguous_dma(reason="one value a partition and block of query rows"):
             nc.gpsimd.dma_start(th_cols[:], th.rearrange("(b p) o -> p (b o)", p=P))
             nc.sync.dma_start(val_pool[0][:], vals_dealt[:, 0, :])
             nc.sync.dma_start(val_pool[1][:], vals_dealt[:, 1, :])
@@ -86,7 +98,10 @@ def tile_attend_ttsoftthreshold_pl_kernel(
             nc.sync.dma_start(val_pool[j][:], vals_dealt[:, j, :])
 
         def round_and_interleave(copy, grouped, raw):
-            copy(grouped.rearrange("p (c i) t -> p c t i", i=4), raw.rearrange("p t (c i) -> p c t i", i=4))
+            copy(grouped.rearrange("p (c i) t -> p c t i", i=LINE), raw.rearrange("p t (c i) -> p c t i", i=LINE))
+
+        def negate(out, in_):
+            nc.scalar.activation(out, in_, ACT.Copy, scale=-1.0)
 
         def quantise(codes, scales, grouped):
             nc.vector.quantize_mx(codes.bitcast(FP8X4), scales, grouped.rearrange("p c t -> p (c t)"))
@@ -95,14 +110,17 @@ def tile_attend_ttsoftthreshold_pl_kernel(
         nc.vector.tensor_copy(key_words[:], key_word_pool[:].indirect(offsets[:]))
         key_scales = sbuf("key_scales", [P, I], U8)
         nc.vector.tensor_copy(key_scales[:], key_scale_pool[:].indirect(offsets[:]))
-        query_grouped = placed(8, 0, "query_grouped", [P, Q, PACK], BF16)
+        query_grouped = sbuf("query_grouped", [P, Q, PACK], BF16)
         query_codes = sbuf("query_codes", [P, Q], U32)
         query_scales = sbuf("query_scales", [P, Q], U8)
         for b in range(BLOCKS):
-            round_and_interleave(nc.scalar.copy, query_grouped[:, cols(b), :], query_raw[:, :, cols(b)])
+            round_and_interleave(negate, query_grouped[:, cols(b), :], query_raw[:, :, cols(b)])
             quantise(query_codes[:, cols(b)], query_scales[:, cols(b)], query_grouped[:, cols(b), :])
-        dquery_grouped = placed(8, 0, "dquery_grouped", [P, Q, PACK], BF16)
-        round_and_interleave(nc.vector.tensor_copy, dquery_grouped[:], dquery_raw[:])
+        dquery_grouped = placed(SIGMOIDS, 0, "dquery_grouped", [P, Q, PACK], BF16)
+        round_and_interleave(nc.scalar.copy, dquery_grouped[:], dquery_raw[:])
+        dquery_codes = sbuf("dquery_codes", [P, Q], U32)
+        dquery_scales = sbuf("dquery_scales", [P, Q], U8)
+        quantise(dquery_codes[:], dquery_scales[:], dquery_grouped[:])
 
         def scores(codes, scales, tag):
             bank = psum.tile([P, I], F32, name=tag, tag=tag)
@@ -117,36 +135,24 @@ def tile_attend_ttsoftthreshold_pl_kernel(
             )
             return bank
 
-        a = [scores(query_codes[:, cols(b)], query_scales[:, cols(b)], "score") for b in range(BLOCKS)]
-
-        x = per_block("x", [P, I], F32)
-        x_sum = per_block("x_sum", [P, 1], F32)
-        x_sum_reserve = per_block("x_sum_reserve", [P, 1], F32)
-        sig = [sbuf("sig0", [P, I], F32), placed(PACK, 0, "sig1", [P, I], F32)]
-        log_sig = per_block("log_sig", [P, I], F32)
-        log_sig_sum = per_block("log_sig_sum", [P, 1], F32)
-        denom = per_block("denom", [P, 1], F32)
-        neg_part = per_block("neg_part", [P, I], F32)
-        tp_sum = per_block("tp_sum", [P, 1], F32)
-        share = per_block("share", [P, 1], F32)
-
-        for b in range(BLOCKS):
-            nc.vector.scalar_tensor_tensor(
-                x[b][:], a[b][:], th_cols[:, b : b + 1], floor[b][:].to_broadcast([P, I]),
-                ALU.subtract, ALU.max, accum_out=x_sum[b][:],
-            )
-            nc.scalar.activation(sig[b][:], x[b][:], ACT.Sigmoid)
-            nc.gpsimd.tensor_tensor(x_sum_reserve[b][:], x_sum[b][:], reserve_cols[:, b : b + 1], ALU.add)
-        dquery_codes = placed(7, 0, "dquery_codes", [P, Q], U32)
-        dquery_scales = sbuf("dquery_scales", [P, Q], U8)
-        quantise(dquery_codes[:], dquery_scales[:], dquery_grouped[:])
+        neg_a = [scores(query_codes[:, cols(b)], query_scales[:, cols(b)], "score") for b in range(BLOCKS)]
         ta = [scores(dquery_codes[:, cols(b)], dquery_scales[:, cols(b)], "dscore") for b in range(BLOCKS)]
+
+        neg_th = [placed(LOGS, ROW_BYTES * (1 - b), "neg_th%d" % b, [P, 1], F32) for b in range(BLOCKS)]
+        co_sig = [placed(QUERIES, 0, "co_sig0", [P, I], F32), placed(ROUNDED, 0, "co_sig1", [P, I], F32)]
+        sig = [placed(SIGMOIDS, ROW_BYTES * (b + 1), "sig%d" % b, [P, I], F32) for b in range(BLOCKS)]
         for b in range(BLOCKS):
-            nc.scalar.activation(log_sig[b][:], sig[b][:], ACT.Ln, accum_out=log_sig_sum[b][:])
-            nc.scalar.activation(
-                denom[b][:], log_sig_sum[b][:], ACT.Identity, bias=x_sum_reserve[b][:], scale=-1.0
-            )
-            nc.gpsimd.tensor_tensor(neg_part[b][:], log_sig[b][:], x[b][:], ALU.subtract)
+            nc.gpsimd.tensor_scalar(neg_th[b][:], th_cols[:, b : b + 1], -1.0, 0.0, ALU.mult, ALU.add)
+            nc.scalar.activation(co_sig[b][:], neg_a[b][:], ACT.Sigmoid, bias=th_cols[:, b : b + 1])
+        for b in range(BLOCKS):
+            nc.scalar.activation(sig[b][:], neg_a[b][:], ACT.Sigmoid, bias=neg_th[b][:], scale=-1.0)
+        log_co_sig = [placed(LOGS, 2 * ROW_BYTES * b, "log_co_sig%d" % b, [P, I], F32) for b in range(BLOCKS)]
+        for b in range(BLOCKS):
+            nc.scalar.activation(log_co_sig[b][:], co_sig[b][:], ACT.Ln, bias=guard[:])
+        tp_sum = per_block("tp_sum", [P, 1], F32)
+        neg_part_sum = per_block("neg_part_sum", [P, 1], F32)
+        denom = per_block("denom", [P, 1], F32)
+        share = per_block("share", [P, 1], F32)
 
         def turn(rows):
             words = rows[:].bitcast(F32)
@@ -162,30 +168,52 @@ def tile_attend_ttsoftthreshold_pl_kernel(
         def group(grouped, turned):
             nc.scalar.copy(grouped.bitcast(F32), turned[:].rearrange("p u m -> p m u"))
 
-        val_turned = [gather_values(sbuf("picked0", [P, I], BF16), 0)]
-        tp = [placed(0, 2048 * b, "tp%d" % b, [P, I], F32) for b in range(BLOCKS)]
-        for b in range(BLOCKS):
+        def tangent_part(out, b):
             nc.vector.scalar_tensor_tensor(
-                tp[b][:], ta[b][:], 1.0, sig[b][:], ALU.mult, ALU.mult, accum_out=tp_sum[b][:]
+                out[:], ta[b][:], 1.0, sig[b][:], ALU.mult, ALU.mult, accum_out=tp_sum[b][:]
             )
+            return out
+
+        val_turned = [gather_values(placed(SIGMOIDS, 0, "picked0", [P, I], BF16), 0)]
+        tp = [tangent_part(placed(0, 0, "tp0", [P, I], F32), 0)]
         factor_rows = psum.tile([P, PACK, P], F32, name="factor_rows", tag="dscore")
         for t in range(PACK):
             nc.tensor.transpose(factor_rows[:, t, :], factor_cols[:, t : t + 1].to_broadcast([P, P]), identity[:])
-        val_turned.append(gather_values(sbuf("picked1", [P, I], BF16), 1))
-        val_grouped = placed(PACK, 0, "val_grouped", [P, PACK * P, PACK], BF16)
-        for j in range(2):
-            group(val_grouped[:, cols(j), :], val_turned[j])
-        inv_denom = [placed(1, 64 * b, "inv_denom%d" % b, [P, 1], F32) for b in range(BLOCKS)]
-        for b in range(BLOCKS):
-            nc.vector.reciprocal(inv_denom[b][:], denom[b][:])
-            nc.scalar.activation(share[b][:], tp_sum[b][:], ACT.Copy, scale=inv_denom[b][:])
-        val_turned.append(gather_values(sbuf("picked2", [P, I], BF16), 2))
-        group(val_grouped[:, cols(2), :], val_turned[2])
+        val_turned.append(gather_values(placed(SIGMOIDS, ROW_BYTES, "picked1", [P, I], BF16), 1))
 
-        numerator = [placed(2, 2048 * b, "numerator%d" % b, [P, I], F32) for b in range(BLOCKS)]
+        rounded_pool = placed(ROUNDED, 0, "rounded_pool", [P, T], BF16)
+        nc.scalar.activation(rounded_pool[:], val_pool[SCALAR_PLANE][:], ACT.Copy)
+        picked2 = sbuf("picked2", [P, I], BF16)
+        nc.scalar.activation(picked2[:], rounded_pool[:].indirect(offsets[:]), ACT.Copy)
+        val_turned.append(turn(picked2))
+        val_grouped = placed(ROUNDED, ROW_BYTES, "val_grouped", [P, PACK * P, PACK], BF16)
+        for j in range(SCALAR_PLANE):
+            group(val_grouped[:, cols(j), :], val_turned[j])
+
+        neg_part = [placed(1, ROW_BYTES * b, "neg_part%d" % b, [P, I], F32) for b in range(BLOCKS)]
+        for b in range(BLOCKS):
+            nc.vector.scalar_tensor_tensor(
+                neg_part[b][:], neg_a[b][:], th_cols[:, b : b + 1], log_co_sig[b][:], ALU.add, ALU.min,
+                accum_out=neg_part_sum[b][:],
+            )
+            nc.gpsimd.tensor_scalar(
+                denom[b][:], neg_part_sum[b][:], -1.0, reserve_cols[:, b : b + 1], ALU.mult, ALU.add
+            )
+
+        inv_denom = per_block("inv_denom", [P, 1], F32)
+
+        def normalise(b):
+            nc.vector.reciprocal(inv_denom[b][:], denom[b][:])
+            nc.gpsimd.tensor_scalar(share[b][:], tp_sum[b][:], inv_denom[b][:], 0.0, ALU.mult, ALU.add)
+
+        normalise(0)
+        tp.append(tangent_part(placed(LOGS, 2 * ROW_BYTES, "tp1", [P, I], F32), 1))
+        normalise(1)
+
+        numerator = [placed(NUMERATORS, ROW_BYTES * b, "numerator%d" % b, [P, I], F32) for b in range(BLOCKS)]
         for b in range(BLOCKS):
             nc.vector.scalar_tensor_tensor(numerator[b][:], neg_part[b][:], share[b][:], tp[b][:], ALU.mult, ALU.add)
-        weights_grouped = sbuf("weights_grouped", [P, Q, PACK], BF16)
+        weights_grouped = placed(ROUNDED, 0, "weights_grouped", [P, Q, PACK], BF16)
         for b in range(BLOCKS):
             weights = sbuf("weights%d" % b, [P, I], BF16)
             nc.vector.scalar_tensor_tensor(
@@ -197,20 +225,22 @@ def tile_attend_ttsoftthreshold_pl_kernel(
                 ALU.mult,
             )
             group(weights_grouped[:, cols(b), :], turn(weights))
+            if b == 0:
+                group(val_grouped[:, cols(SCALAR_PLANE), :], val_turned[SCALAR_PLANE])
         last = PACK - 1
-        group(val_grouped[:, cols(last), :], gather_values(placed(2, 0, "picked3", [P, I], BF16), last))
+        group(val_grouped[:, cols(last), :], gather_values(placed(NUMERATORS, 0, "picked3", [P, I], BF16), last))
 
-        val_codes = placed(3, 0, "val_codes", [P, PACK * P], U32)
+        val_codes = placed(last, 0, "val_codes", [P, PACK * P], U32)
         val_scales = sbuf("val_scales", [P, PACK * P], U8)
-        weights_codes = placed(3, 2048, "weights_codes", [P, Q], U32)
+        weights_codes = placed(last, PACK * P * 4, "weights_codes", [P, Q], U32)
         weights_scales = sbuf("weights_scales", [P, Q], U8)
 
         def quantise_values(part):
             quantise(val_codes[:, part], val_scales[:, part], val_grouped[:, part, :])
 
-        quantise_values(slice(0, 2 * P))
-        quantise_values(cols(2))
+        quantise_values(slice(0, SCALAR_PLANE * P))
         quantise(weights_codes[:], weights_scales[:], weights_grouped[:])
+        quantise_values(cols(SCALAR_PLANE))
         quantise_values(cols(last))
 
         staged = sbuf("staged", [P, PACK, Q], F32)
@@ -246,7 +276,4 @@ def tile_attend_ttsoftthreshold_pl_kernel(
         nc.sync.dma_start(out_1[0].rearrange("p c t -> p (c t)").bitcast(I32), out_codes[:].bitcast(I32))
         for quad in range(QUADRANTS):
             queue = nc.sync if quad % 2 == 0 else nc.scalar
-            queue.dma_start(
-                out_2[0, 4 * quad : 4 * quad + 4, :].bitcast(I32),
-                out_scales[32 * quad : 32 * quad + 4, :].bitcast(I32),
-            )
+            queue.dma_start(dram_rows(out_2, quad), live_rows(out_scales, quad))

from contextlib import ExitStack

import concourse.mybir as mybir

D, E, T, I, Q = 512, 512, 2048, 512, 256
FLOPS = 2 * (2 * D * Q * I + I * E * Q)

F32 = mybir.dt.float32
BF16 = mybir.dt.bfloat16
I32 = mybir.dt.int32
U32 = mybir.dt.uint32
U16 = mybir.dt.uint16
U8 = mybir.dt.uint8
FP8X4 = mybir.dt.float8_e4m3fn_x4
FP4X4 = mybir.dt.float4_e2m1fn_x4
ALU = mybir.AluOpType
ACT = mybir.ActivationFunctionType

P = 128
PACK = 4
BLOCKS = Q // P
QUADRANTS = 4
QUADRANT_ROWS = P // QUADRANTS
SCALE_ROWS = 4
LINE = 4
GUARD_SCORE = -40.0

REGION_BYTES = T * 4
ROW_BYTES = I * 4
ROUNDED, QUERIES, COLUMNS, SIGMOIDS, LOGS, NUMERATORS = range(PACK, PACK + 6)
SCALAR_PLANE = 2


def tile_attend_ttsoftthreshold_pl_kernel(
    tc, query, dquery, keys_words, keys_scales, th, reserve, slot_factor, vals, offs, out_0, out_1, out_2
):
    nc = tc.nc
    with ExitStack() as ctx:
        held = ctx.enter_context(tc.tile_pool(name="held", bufs=1))
        reuse = ctx.enter_context(tc.tile_pool(name="reuse", bufs=1))
        psum = ctx.enter_context(tc.psum_pool(name="psum", bufs=2))

        def sbuf(name, shape, dtype):
            return held.tile(shape, dtype, name=name, align_bytes=64)

        def placed(region, at, name, shape, dtype):
            return reuse.tile(shape, dtype, name=name, align_bytes=64, offset=region * REGION_BYTES + at)

        def per_block(name, shape, dtype):
            return [sbuf("%s%d" % (name, b), shape, dtype) for b in range(BLOCKS)]

        def cols(n):
            return slice(n * P, (n + 1) * P)

        def live_rows(scale_tile, quad):
            return scale_tile[QUADRANT_ROWS * quad : QUADRANT_ROWS * quad + SCALE_ROWS, :].bitcast(I32)

        def dram_rows(scale_rows, quad):
            return scale_rows[0, SCALE_ROWS * quad : SCALE_ROWS * (quad + 1), :].bitcast(I32)

        offsets = held.tile([P, I // 16], U16, name="offsets")
        nc.sync.dma_start(offsets[:], offs)
        key_word_pool = sbuf("key_word_pool", [P, T], U16)
        nc.sync.dma_start(key_word_pool[:].bitcast(I32), keys_words[0].bitcast(I32))
        key_scale_pool = sbuf("key_scale_pool", [P, T], U8)
        nc.gpsimd.memset(key_scale_pool[:].bitcast(I32), 0)
        for quad in range(QUADRANTS):
            nc.sync.dma_start(live_rows(key_scale_pool, quad), dram_rows(keys_scales, quad))

        zeros = placed(0, 0, "zeros", [P, (COLUMNS + 1) * T], F32)
        nc.vector.memset(zeros[:, :P], 0.0)
        identity = sbuf("identity", [P, P], F32)
        nc.gpsimd.affine_select(
            out=identity[:], in_=zeros[:, :P], compare_op=ALU.not_equal, fill=1.0, base=0,
            pattern=[[-1, P]], channel_multiplier=1,
        )
        guard_score = sbuf("guard_score", [P, 1], F32)
        nc.vector.memset(guard_score[:], GUARD_SCORE)
        guard = sbuf("guard", [P, 1], F32)
        nc.scalar.activation(guard[:], guard_score[:], ACT.Sigmoid)

        query_raw = placed(QUERIES, PACK * Q * 4, "query_raw", [P, PACK, Q], F32)
        nc.sync.dma_start(query_raw[:], query.rearrange("(p t) q -> p t q", t=PACK))
        dquery_raw = placed(QUERIES, 0, "dquery_raw", [P, PACK, Q], F32)
        nc.sync.dma_start(dquery_raw[:], dquery.rearrange("(p t) q -> p t q", t=PACK))
        val_pool = [placed(j, 0, "val_pool%d" % j, [P, T], F32) for j in range(PACK)]
        vals_dealt = vals.rearrange("(m j) t -> m j t", j=PACK)
        th_cols = sbuf("th_cols", [P, BLOCKS], F32)
        reserve_cols = placed(COLUMNS, 64, "reserve_cols", [P, BLOCKS], F32)
        factor_cols = placed(COLUMNS, 128, "factor_cols", [P, PACK], F32)
        with nc.allow_non_contiguous_dma(reason="one value a partition and block of query rows"):
            nc.gpsimd.dma_start(th_cols[:], th.rearrange("(b p) o -> p (b o)", p=P))
            nc.sync.dma_start(val_pool[0][:], vals_dealt[:, 0, :])
            nc.sync.dma_start(val_pool[1][:], vals_dealt[:, 1, :])
            nc.sync.dma_start(reserve_cols[:], reserve.rearrange("(b p) o -> p (b o)", p=P))
        nc.sync.dma_start(factor_cols[:], slot_factor.rearrange("o (p t) -> p (o t)", t=PACK))
        for j in range(2, PACK):
            nc.sync.dma_start(val_pool[j][:], vals_dealt[:, j, :])

        def round_and_interleave(copy, grouped, raw):
            copy(grouped.rearrange("p (c i) t -> p c t i", i=LINE), raw.rearrange("p t (c i) -> p c t i", i=LINE))

        def negate(out, in_):
            nc.scalar.activation(out, in_, ACT.Copy, scale=-1.0)

        def quantise(codes, scales, grouped):
            nc.vector.quantize_mx(codes.bitcast(FP8X4), scales, grouped.rearrange("p c t -> p (c t)"))

        key_words = sbuf("key_words", [P, I], U16)
        nc.vector.tensor_copy(key_words[:], key_word_pool[:].indirect(offsets[:]))
        key_scales = sbuf("key_scales", [P, I], U8)
        nc.vector.tensor_copy(key_scales[:], key_scale_pool[:].indirect(offsets[:]))
        query_grouped = sbuf("query_grouped", [P, Q, PACK], BF16)
        query_codes = sbuf("query_codes", [P, Q], U32)
        query_scales = sbuf("query_scales", [P, Q], U8)
        for b in range(BLOCKS):
            round_and_interleave(negate, query_grouped[:, cols(b), :], query_raw[:, :, cols(b)])
            quantise(query_codes[:, cols(b)], query_scales[:, cols(b)], query_grouped[:, cols(b), :])
        dquery_grouped = placed(SIGMOIDS, 0, "dquery_grouped", [P, Q, PACK], BF16)
        round_and_interleave(nc.scalar.copy, dquery_grouped[:], dquery_raw[:])
        dquery_codes = sbuf("dquery_codes", [P, Q], U32)
        dquery_scales = sbuf("dquery_scales", [P, Q], U8)
        quantise(dquery_codes[:], dquery_scales[:], dquery_grouped[:])

        def scores(codes, scales, tag):
            bank = psum.tile([P, I], F32, name=tag, tag=tag)
            nc.tensor.matmul_mx(
                bank[:],
                lhsT=codes.bitcast(FP8X4),
                lhsT_scale=scales,
                rhs=key_words[:].bitcast(FP4X4),
                rhs_scale=key_scales[:],
                start=True,
                stop=True,
            )
            return bank

        neg_a = [scores(query_codes[:, cols(b)], query_scales[:, cols(b)], "score") for b in range(BLOCKS)]
        ta = [scores(dquery_codes[:, cols(b)], dquery_scales[:, cols(b)], "dscore") for b in range(BLOCKS)]

        neg_th = [placed(LOGS, ROW_BYTES * (1 - b), "neg_th%d" % b, [P, 1], F32) for b in range(BLOCKS)]
        co_sig = [placed(QUERIES, 0, "co_sig0", [P, I], F32), placed(ROUNDED, 0, "co_sig1", [P, I], F32)]
        sig = [placed(SIGMOIDS, ROW_BYTES * (b + 1), "sig%d" % b, [P, I], F32) for b in range(BLOCKS)]
        for b in range(BLOCKS):
            nc.gpsimd.tensor_scalar(neg_th[b][:], th_cols[:, b : b + 1], -1.0, 0.0, ALU.mult, ALU.add)
            nc.scalar.activation(co_sig[b][:], neg_a[b][:], ACT.Sigmoid, bias=th_cols[:, b : b + 1])
        for b in range(BLOCKS):
            nc.scalar.activation(sig[b][:], neg_a[b][:], ACT.Sigmoid, bias=neg_th[b][:], scale=-1.0)
        log_co_sig = [placed(LOGS, 2 * ROW_BYTES * b, "log_co_sig%d" % b, [P, I], F32) for b in range(BLOCKS)]
        for b in range(BLOCKS):
            nc.scalar.activation(log_co_sig[b][:], co_sig[b][:], ACT.Ln, bias=guard[:])
        tp_sum = per_block("tp_sum", [P, 1], F32)
        neg_part_sum = per_block("neg_part_sum", [P, 1], F32)
        denom = per_block("denom", [P, 1], F32)
        share = per_block("share", [P, 1], F32)

        def turn(rows):
            words = rows[:].bitcast(F32)
            turned = psum.tile([P, 2, P], F32, name="turned", tag="turned", bufs=4)
            for u in range(2):
                nc.tensor.transpose(turned[:, u, :], words[:, u::2], identity[:])
            return turned

        def gather_values(picked, j):
            nc.vector.tensor_copy(picked[:], val_pool[j][:].indirect(offsets[:]))
            return turn(picked)

        def group(grouped, turned):
            nc.scalar.copy(grouped.bitcast(F32), turned[:].rearrange("p u m -> p m u"))

        def tangent_part(out, b):
            nc.vector.scalar_tensor_tensor(
                out[:], ta[b][:], 1.0, sig[b][:], ALU.mult, ALU.mult, accum_out=tp_sum[b][:]
            )
            return out

        val_turned = [gather_values(placed(SIGMOIDS, 0, "picked0", [P, I], BF16), 0)]
        tp = [tangent_part(placed(0, 0, "tp0", [P, I], F32), 0)]
        factor_rows = psum.tile([P, PACK, P], F32, name="factor_rows", tag="dscore")
        for t in range(PACK):
            nc.tensor.transpose(factor_rows[:, t, :], factor_cols[:, t : t + 1].to_broadcast([P, P]), identity[:])
        val_turned.append(gather_values(placed(SIGMOIDS, ROW_BYTES, "picked1", [P, I], BF16), 1))

        rounded_pool = placed(ROUNDED, 0, "rounded_pool", [P, T], BF16)
        nc.scalar.activation(rounded_pool[:], val_pool[SCALAR_PLANE][:], ACT.Copy)
        picked2 = sbuf("picked2", [P, I], BF16)
        nc.scalar.activation(picked2[:], rounded_pool[:].indirect(offsets[:]), ACT.Copy)
        val_turned.append(turn(picked2))
        val_grouped = placed(ROUNDED, ROW_BYTES, "val_grouped", [P, PACK * P, PACK], BF16)
        for j in range(SCALAR_PLANE):
            group(val_grouped[:, cols(j), :], val_turned[j])

        neg_part = [placed(1, ROW_BYTES * b, "neg_part%d" % b, [P, I], F32) for b in range(BLOCKS)]
        for b in range(BLOCKS):
            nc.vector.scalar_tensor_tensor(
                neg_part[b][:], neg_a[b][:], th_cols[:, b : b + 1], log_co_sig[b][:], ALU.add, ALU.min,
                accum_out=neg_part_sum[b][:],
            )
            nc.gpsimd.tensor_scalar(
                denom[b][:], neg_part_sum[b][:], -1.0, reserve_cols[:, b : b + 1], ALU.mult, ALU.add
            )

        inv_denom = per_block("inv_denom", [P, 1], F32)

        def normalise(b):
            nc.vector.reciprocal(inv_denom[b][:], denom[b][:])
            nc.gpsimd.tensor_scalar(share[b][:], tp_sum[b][:], inv_denom[b][:], 0.0, ALU.mult, ALU.add)

        normalise(0)
        tp.append(tangent_part(placed(LOGS, 2 * ROW_BYTES, "tp1", [P, I], F32), 1))
        normalise(1)

        numerator = [placed(NUMERATORS, ROW_BYTES * b, "numerator%d" % b, [P, I], F32) for b in range(BLOCKS)]
        for b in range(BLOCKS):
            nc.vector.scalar_tensor_tensor(numerator[b][:], neg_part[b][:], share[b][:], tp[b][:], ALU.mult, ALU.add)
        weights_grouped = placed(ROUNDED, 0, "weights_grouped", [P, Q, PACK], BF16)
        for b in range(BLOCKS):
            weights = sbuf("weights%d" % b, [P, I], BF16)
            nc.vector.scalar_tensor_tensor(
                weights[:].rearrange("q (s t) -> q s t", t=PACK),
                numerator[b][:].rearrange("q (s t) -> q s t", t=PACK),
                inv_denom[b][:],
                factor_rows[:].rearrange("q t s -> q s t"),
                ALU.mult,
                ALU.mult,
            )
            group(weights_grouped[:, cols(b), :], turn(weights))
            if b == 0:
                group(val_grouped[:, cols(SCALAR_PLANE), :], val_turned[SCALAR_PLANE])
        last = PACK - 1
        group(val_grouped[:, cols(last), :], gather_values(placed(NUMERATORS, 0, "picked3", [P, I], BF16), last))

        val_codes = placed(last, 0, "val_codes", [P, PACK * P], U32)
        val_scales = sbuf("val_scales", [P, PACK * P], U8)
        weights_codes = placed(last, PACK * P * 4, "weights_codes", [P, Q], U32)
        weights_scales = sbuf("weights_scales", [P, Q], U8)

        def quantise_values(part):
            quantise(val_codes[:, part], val_scales[:, part], val_grouped[:, part, :])

        quantise_values(slice(0, SCALAR_PLANE * P))
        quantise(weights_codes[:], weights_scales[:], weights_grouped[:])
        quantise_values(cols(SCALAR_PLANE))
        quantise_values(cols(last))

        staged = sbuf("staged", [P, PACK, Q], F32)
        out_dealt = out_0.rearrange("(m j) q -> m j q", j=PACK)

        def product(planes, tag, copy):
            result = psum.tile([P, len(planes), Q], F32, name="result", tag=tag)
            for n, j in enumerate(planes):
                nc.tensor.matmul_mx(
                    result[:, n, :],
                    lhsT=val_codes[:, cols(j)].bitcast(FP8X4),
                    lhsT_scale=val_scales[:, cols(j)],
                    rhs=weights_codes[:].bitcast(FP8X4),
                    rhs_scale=weights_scales[:],
                    start=True,
                    stop=True,
                )
            copy(staged[:, planes.start : planes.stop, :], result[:])

        product(range(0, 2), "score", nc.scalar.copy)
        product(range(2, last), "score", nc.scalar.copy)
        nc.sync.dma_start(out_dealt[:, :last, :], staged[:, :last, :])
        product(range(last, PACK), "dscore", nc.vector.tensor_copy)
        nc.sync.dma_start(out_dealt[:, last, :], staged[:, last, :])

        out_grouped = sbuf("out_grouped", [P, Q, PACK], BF16)
        out_codes = sbuf("out_codes", [P, Q], U32)
        out_scales = sbuf("out_scales", [P, Q], U8)
        for b, copy in enumerate((nc.vector.tensor_copy, nc.scalar.copy)):
            round_and_interleave(copy, out_grouped[:, cols(b), :], staged[:, :, cols(b)])
        for b in range(BLOCKS):
            quantise(out_codes[:, cols(b)], out_scales[:, cols(b)], out_grouped[:, cols(b), :])
        nc.sync.dma_start(out_1[0].rearrange("p c t -> p (c t)").bitcast(I32), out_codes[:].bitcast(I32))
        for quad in range(QUADRANTS):
            queue = nc.sync if quad % 2 == 0 else nc.scalar
            queue.dma_start(dram_rows(out_2, quad), live_rows(out_scales, quad))
